import numpy as np, ml_dtypes
CORES = [25,29,65,69,153,157,193,197]
N = 8
import mx_ref
BF = ml_dtypes.bfloat16
def gentries(a):
    return np.ascontiguousarray(a.reshape(8, 16, -1).transpose(0, 2, 1)).reshape(8, -1)
def gtable(e):
    e = np.asarray(e); return np.ascontiguousarray(e.reshape(8, -1, 16).transpose(0, 2, 1)).reshape(128, -1).astype(np.int32)
def gcols(t, e):
    v = np.concatenate([t.reshape(8, 16, -1, 4), np.zeros((8, 16, 1, 4), BF)], axis=2)
    return np.ascontiguousarray(np.stack([v[g][:, e[g]] for g in range(8)])).reshape(128, -1)
def tile(rs):
    return np.stack(rs, axis=2).reshape(128, -1).astype(BF)
def pick(q, e):
    c = np.concatenate([q[0].reshape(128, -1, 4), np.zeros((128, 1, 4), np.uint8)], axis=1); s = np.concatenate([q[1], np.ones((16, 1), np.uint8)], axis=1)
    return (np.ascontiguousarray(c[:, e].reshape(128, -1)), np.ascontiguousarray(s[:, e]))
def join(*qs):
    return (np.concatenate([q[0] for q in qs], axis=1), np.concatenate([q[1] for q in qs], axis=1))
def put(q, e, v):
    c, s = q[0].reshape(128, -1, 4).copy(), q[1].copy(); c[:, e] = v[0].reshape(128, -1, 4); s[:, e] = v[1]
    return (c.reshape(128, -1), s)
def pk(c, s):
    return (np.ascontiguousarray(c), mx_ref.live(s))
def emit(q):
    return q[0], q[1]
def packed(v, rng):
    q = [mx_ref.quantize(np.ascontiguousarray(v[r])) for r in range(N)]
    return np.stack([a for a, b in q]), np.stack([mx_ref.plane(b, rng) for a, b in q])
def values_of_codes():
    e, c = np.zeros((128, 128, 4), np.float32), np.zeros((128, 2, 4), np.uint8)
    e[np.arange(128), np.arange(128), 0] = 1
    c[:127, :, 0] = np.arange(256).reshape(2, 128).T[:127]
    return mx_ref.matmul(mx_ref.quantize(e.reshape(128, 512).astype(BF)), (c.reshape(128, 8), np.full((16, 2), 127, np.uint8))).T.reshape(-1).astype(np.float64)
CODE_VALUE, SCALE_VALUE = values_of_codes(), 2.0 ** (np.arange(256) - 127.0)
def decode(q):
    return (CODE_VALUE[q[0]].reshape(16, 8, -1, 4) * SCALE_VALUE[q[1]][:, None, :, None] + 0.0).reshape(128, -1).astype(np.float32)
def f(rng, *shape):
    return mx_ref.flush((rng.standard_normal(shape, dtype=np.float32) * np.exp2(rng.integers(-2, 3, shape[:-1] + (1,)))).astype(BF))
def wide(rng, *shape, cols=0):
    v = rng.standard_normal(shape, dtype=np.float32) * np.exp2(rng.integers(-12, 13, shape)).astype(np.float32)
    if cols: v *= np.repeat(np.exp2(rng.integers(-cols, cols + 1, shape[:-2] + (1, shape[-1] // 4))) * (rng.random(shape[:-2] + (1, shape[-1] // 4)) > 0.0625), 4, axis=-1).astype(np.float32)
    return mx_ref.flush(v.astype(BF))
C, H = 352, 176
STEP = [4, 1, 2]
PLACES = np.arange(C)
def numbers_of(rng):
    return {"x": np.array(f(rng, N, 128, 4 * C)), "u": np.array(f(rng, N, 128, 512)), "v": np.array(f(rng, N, 128, 512))}
def drawn(rng):
    o = rng.permuted(np.tile(PLACES, (N, 8, 3, 1)), axis=3)
    k = np.zeros_like(o)
    np.put_along_axis(k, o, o.reshape(N, 8, 3, H, 2)[..., ::-1].reshape(N, 8, 3, C), axis=3)
    e = np.tile(PLACES, (N, 8, 1))
    return rng.permuted(e, axis=2), rng.permuted(e, axis=2), k
def stored(p, e, k):
    return {"pp": np.stack([gtable(p[r]) for r in range(N)]), "rf": np.stack([gtable(e[r]) for r in range(N)]), "pr": np.stack([gtable(k[r].reshape(8, 3 * C)) for r in range(N)])}
def layers(rng, still=[]):
    w = np.array(f(rng, N, 128, 2048)).reshape(N, 8, 16, 4, 8, 16, 4)
    for i in still:
        w[:, :, i] = 0
        w[:, :, :, :, :, i] = 0
    return w
def weights(rng, w):
    c, s = packed(np.ascontiguousarray(w).reshape(N, 128, 2048), rng)
    return {"wc": c, "ws": s}
def scoring(d):
    u = d["u"].reshape(N, 128, 128, 4)
    u[:, :, ::16] = 0
    u[:, :, 1::16] = 0
    return u
def setup_inputs(rng):
    return {**numbers_of(rng), **stored(*drawn(rng)), **weights(rng, layers(rng))}
def setup_inputs_ties(rng):
    d = numbers_of(rng)
    p, e, k = drawn(rng)
    o = rng.permutation(N)
    k[o[3], :4] = k[o[3], :4, :1]
    a, b = rng.integers(-1, 2, (2, N, 8, C))
    a[o[0]] = 0
    a[o[1]] = 1
    b[o[1], :4] = 1
    b[o[1], 4:] = 0
    for g in range(4): a[o[3], g, p[o[3], g]] = np.where(PLACES < k[o[3], g, 0], 1, -rng.integers(0, 2, C))
    x = d["x"].reshape(N, 8, 16, C, 4)
    x[:, :, 0] = 0
    x[:, :, 0, :, 0] = a.astype(np.float32).astype(BF)
    x[:, :, 0, :, 1] = b.astype(np.float32).astype(BF)
    u = scoring(d)
    for h in range(0, 128, 16):
        u[:, h, h, 0] = 1
        u[:, h, h + 1, 1] = 1
    return {"x": x.reshape(N, 128, 4 * C), "u": u.reshape(N, 128, 512), "v": d["v"], **stored(p, rng.integers(0, C, (N, 8, C)), k), **weights(rng, layers(rng, [0]))}
def setup_inputs_near(rng):
    d = numbers_of(rng)
    o = rng.permutation(N)
    z = int(np.argmax(o))
    k = np.where(o % 2 == 0, 2.0 ** -30, 1.0)
    x = np.zeros((N, 8, 16, C, 4))
    for i in (0, 2):
        s = rng.integers(-1, 2, (N, 8, C)) * k[:, None, None]
        x[:, :, i, :, 0] = 1.125 * s
        x[:, :, i + 1, :, 0] = -1.25 * s
    for r in range(N):
        at_ = [0, C - 1, int(rng.integers(C)), int(rng.integers(C))]
        for g, j in zip(rng.permutation(8)[:4], at_): x[r, g, 0, j, 0] = 2.0 ** 30 * rng.choice([-1.0, 1.0])
    x[:, :, 8:] = rng.choice([-1.0, 1.0], (N, 8, 8, C, 4)) * (1 + 0.125 * rng.integers(0, 8, (N, 8, 8, C, 4))) * 2.0 ** -30
    x[z, :, :8] = 0
    x[:, :, 7, :, 0] = 2.0 ** -30
    x[:, :, 8, :, 3] = 2.0 ** -30
    u = scoring(d)
    w = layers(rng)
    w[:, :, :8] = 0
    w[:, :, :, :, :, :9] = 0
    for h in range(0, 128, 16):
        for i in (0, 1):
            u[:, h + 2 * i, h + i, 0] = (1.125 * k).astype(np.float32).astype(BF)
            u[:, h + 2 * i + 1, h + i, 0] = k.astype(np.float32).astype(BF)
            u[z, :, h + i] = 0
            u[z, h + 5 + i, h + i, 0] = 2.0 ** -30
            w[z, h // 16, 8, 0, h // 16, 5 + i, i] = 2.0 ** -8
    return {"x": x.astype(np.float32).reshape(N, 128, 4 * C).astype(BF), "u": u.reshape(N, 128, 512), "v": d["v"], **stored(*drawn(rng)), **weights(rng, w)}
def setup_inputs_odd(rng):
    d = numbers_of(rng)
    x = (2 * rng.integers(0, 8, (N, 16, 8, C, 4)) + 1) * 2.0 ** -8 * rng.choice([-1.0, 1.0], (N, 16, 8, C, 4))
    x[:, :, 0, :, 0] = 2.0 ** 8 * np.where(rng.random((N, 16, C)) < 0.5, 1.96875, 1.875)
    u = scoring(d)
    for i in (0, 1):
        x[:, ::2, 1 + 2 * i, :, 0] = (8 + rng.integers(0, 2, (N, 8, C))) * 2.0 ** -8
        x[:, ::2, 2 + 2 * i, :, 0] = 8 * 2.0 ** -8
        for h in range(0, 128, 16):
            u[:, h + 1 + 2 * i, h + i, 0] = 1
            u[:, h + 2 + 2 * i, h + i, 0] = -1
    return {"x": x.astype(np.float32).reshape(N, 128, 4 * C).astype(BF), "u": u.reshape(N, 128, 512), "v": d["v"], **stored(*drawn(rng)), **weights(rng, layers(rng, [0, 1, 2, 3, 4, 8]))}
def setup_inputs_ends(rng):
    d = numbers_of(rng)
    p, q, k = drawn(rng)
    o, e = rng.permutation(N) % 4, rng.permutation(N) % 4
    s = rng.choice([-1.0, 1.0], (N, 128, C, 4))
    s[o == 0] = -1
    s[o == 1] = rng.choice([-1.0, 1.0], (N, 1, C, 1))[o == 1]
    x = s * (0.87 + 0.07 * rng.random((N, 128, C, 4))) * 2.0 ** 30
    x[:, 15::16] = 0
    x[o == 3] = 2.0 ** -30
    size = np.where(o == 3, 2.0 ** -30, 2.0 ** 30)
    u = scoring(d)
    for i in (0, 1):
        a = np.stack([rng.permutation(8) % 2 * 2.0 - 1.0 for r in range(N)]) * size[:, None]
        u[:, :, i::16] = a.astype(np.float32).astype(BF)[:, None, :, None]
    v = rng.choice([-1.0, 1.0], (N, 128, 512)) * np.where(o % 2 == 1, 2.0 ** -30, 2.0 ** 30)[:, None, None]
    p[e == 0] = PLACES
    p[e == 1] = PLACES[::-1]
    q[e == 0] = np.where(np.arange(8) % 2 == 0, C - 1, 0)[:, None]
    q[e == 1] = (rng.integers(0, 2, (N, 8, C)) * (C - 1))[e == 1]
    q[e == 2] = PLACES
    q[e == 3] = rng.integers(0, C, (N, 8, C))[e == 3]
    k[e == 0] = PLACES
    k[e == 1] = PLACES[::-1]
    k[e == 2] = PLACES ^ 1
    w = np.zeros((N, 128, 4, 128, 4), np.float32)
    i = np.arange(128)
    for b in range(4): w[:, i, b, i, b] = np.where(o[:, None] == 3, np.where(i % 16 == 15, 2.0 ** 8, 2.0 ** -8), -0.25)
    return {"x": x.astype(np.float32).reshape(N, 128, 4 * C).astype(BF), "u": u.reshape(N, 128, 512), "v": v.astype(np.float32).astype(BF), **stored(p, q, k), **weights(rng, w.astype(BF))}
def setup_inputs_spread(rng):
    d = setup_inputs(rng)
    d["x"] = wide(rng, N, 128, 4 * C, cols=6)
    return d
def check_inputs(d):
    b = []
    for k in ("x", "u", "v"):
        a = np.abs(d[k].astype(np.float32))
        if not (np.isfinite(a).all() and ((a == 0) | (a >= 2.0 ** -30) & (a <= 2.0 ** 30)).all()): b.append("a value of " + k)
    for k in ("pp", "rf", "pr"):
        if not ((d[k] >= 0) & (d[k] < C)).all(): b.append("an entry of " + k)
    none, least, most = [emit(mx_ref.quantize(np.full((128, 16), k, np.float32).astype(BF)))[1][0, 0] for k in (0.0, 2.0 ** -8, 2.0 ** 8)]
    for r in range(N):
        if not (np.sort(gentries(d["pp"][r]), axis=1) == PLACES).all(): b.append("pp: a column not once in a group")
        k = gentries(d["pr"][r]).reshape(8, 3, C)
        if ((k >= 0) & (k < C)).all() and not (np.take_along_axis(k, k, axis=2) == PLACES).all(): b.append("pr: a place that isn't the pair of its pair")
        if ((d["wc"][r] == 0x7F) | (d["wc"][r] == 0xFF)).any(): b.append("wc: a code that is no number")
        s = mx_ref.live(d["ws"][r])
        if ((s != none) & ((s < least) | (s > most))).any(): b.append("ws: a scale out of range")
        if (((d["wc"][r].reshape(16, 8, 512, 4) & 0x7F) != 0) & (s == none)[:, None, :, None]).any(): b.append("wc: a code other than zero under the scale of zeros")
    return b
def at(a, e):
    return np.take_along_axis(a, e, axis=1)
def layer(w, q):
    return tile([mx_ref.matmul(pick(w, np.arange(128 * b, 128 * b + 128)), q) * np.float32(0.03125) for b in range(4)])
def reference(x, u, v, pp, rf, pr, wc, ws):
    qu = [mx_ref.quantize(u[r]) for r in range(N)]
    lay = [pk(wc[r], ws[r]) for r in range(N)]
    place, refs = [gentries(pp[r]) for r in range(N)], [gentries(rf[r]) for r in range(N)]
    pair = [gentries(pr[r]).reshape(8, 3, C) for r in range(N)]
    now = [x[r] for r in range(N)]
    for t, step in enumerate(STEP):
        held, mix = [], []
        for r in range(N):
            q = mx_ref.quantize(now[r])
            s = mx_ref.matmul(qu[r], q)
            sign, mode = s[::16] > 0, s[1::16] > 0
            held.append(decode(q))
            k, here = pair[r][:, t], at(sign, place[r])
            swap = np.where(here == at(here, k), k, PLACES)
            place[r] = at(place[r], swap)
            old = at(refs[r], swap)
            refs[r] = np.where(at(mode, place[r]), at(swap, old), (old + PLACES - swap) % C)
            g = held[r].astype(BF)
            z = gcols(g, place[r]).astype(np.float32) + gcols(g, at(place[r], refs[r])).astype(np.float32)
            mix.append(mx_ref.quantize((z * np.float32(0.5)).astype(BF)))
        for r in range(N):
            h = layer(lay[r], join(pick(mix[r], np.arange(H)), pick(mix[r ^ step], np.arange(H, C))))
            inverse = np.argsort(place[r], axis=1)
            now[r] = (held[r] + gcols(h, at(refs[r ^ step], at(refs[r], inverse))).astype(np.float32)).astype(BF)
    y, pf = np.zeros((N, 128, C), np.float32), np.zeros((N, 8, 2 * C), np.float32)
    oc, osc = np.zeros((N, 128, 4 * C), np.uint8), np.zeros((N, 16, C), np.uint8)
    for r in range(N):
        q = mx_ref.quantize(now[r])
        y[r] = mx_ref.matmul(mx_ref.quantize(v[r]), q)
        pf[r] = np.concatenate([place[r], refs[r]], axis=1)
        oc[r], osc[r] = emit(q)
    return {"y": y, "pf": pf, "oc": oc, "osc": osc}

@@ -1,0 +1,428 @@
+from concourse.bass import DstId, RemoteDMATransfer
+from concourse.mybir import dt, AluOpType, ActivationFunctionType
+
+A, F = AluOpType, ActivationFunctionType
+N, C, H = 8, 352, 176
+STEP = [4, 1, 2]
+CH = [(0, 224), (224, 352)]
+LATE = [False, True]
+BIG = 16384.0
+
+SCRATCH = {
+    "xin": ("sbuf", [128, 4 * C], "bfloat16"), "xt": ("sbuf", [128, 4 * C], "bfloat16"),
+    "ut": ("sbuf", [128, 512], "bfloat16"), "vt": ("sbuf", [128, 512], "bfloat16"),
+    "uq": ("sbuf", [128, 128], "float8_e4m3fn_x4"), "us": ("sbuf", [128, 128], "uint8"),
+    "ua": ("sbuf", [128, 256], "float8_e4m3fn_x4"), "uas": ("sbuf", [128, 256], "uint8"),
+    "vq": ("sbuf", [128, 128], "float8_e4m3fn_x4"), "vs": ("sbuf", [128, 128], "uint8"),
+    "wq": ("sbuf", [128, 512], "float8_e4m3fn_x4"), "wsp": ("sbuf", [128, 512], "uint8"),
+    "one": ("sbuf", [128, 2048], "bfloat16"), "et": ("sbuf", [128, 2048], "bfloat16"),
+    "eq": ("sbuf", [128, 512], "float8_e4m3fn_x4"), "es": ("sbuf", [128, 512], "uint8"),
+    "ppi": ("sbuf", [128, 22], "int32"), "rfi": ("sbuf", [128, 22], "int32"), "pri": ("sbuf", [128, 66], "int32"),
+    "pp16": ("sbuf", [128, 22], "uint16"), "rf16": ("sbuf", [128, 22], "uint16"), "pr16": ("sbuf", [128, 66], "uint16"),
+    "idx": ("sbuf", [128, C], "float32"), "jj": ("sbuf", [128, C], "int32"), "dd": ("sbuf", [128, C], "int32"),
+    "mk": ("sbuf", [128, 2 * C], "float32"), "c1": ("sbuf", [128, C], "float32"),
+    "ck": ("sbuf", [128, C], "float32"), "j16": ("sbuf", [128, C], "int32"), "c01": ("sbuf", [128, C], "float32"),
+    "wt": ("sbuf", [128, 2], "float32"), "uoi": ("sbuf", [128, 16], "int32"), "uo": ("sbuf", [128, 16], "uint16"),
+    "pm": ("sbuf", [128, 66], "int32"), "q16": ("sbuf", [128, 66], "int32"),
+    "qq": ("sbuf", [128, 66], "int32"), "qk": ("sbuf", [128, 66], "float32"),
+    "sa": ("sbuf", [128, C], "bfloat16"), "bw": ("sbuf", [128, 864], "float32"), "am": ("sbuf", [128, C], "float32"),
+    "sE": ("sbuf", [128, C], "float32"), "e3": ("sbuf", [128, 66], "float32"), "sm": ("sbuf", [128, 66], "float32"),
+    "gm": ("sbuf", [128, 2 * C], "float32"), "gs": ("sbuf", [128, 2 * C], "float32"),
+    "tt": ("sbuf", [128, 44], "float32"), "t3": ("sbuf", [128, 22], "int32"),
+    "pkf": ("sbuf", [128, 2 * C], "float32"), "sp": ("sbuf", [128, 2 * C], "float32"),
+    "x1": ("sbuf", [128, 66], "int32"), "xx": ("sbuf", [128, 22], "float32"), "nn": ("sbuf", [128, 22], "int32"),
+    "fsr": ("sbuf", [128, C], "float32"), "hr": ("sbuf", [128, C], "float32"), "ew": ("sbuf", [128, C], "float32"),
+    "esc": ("sbuf", [128, C], "float32"), "ei": ("sbuf", [128, 22], "int32"),
+    "fp": ("sbuf", [128, 4 * C], "bfloat16"), "gp": ("sbuf", [128, 4 * C], "bfloat16"), "bp": ("sbuf", [128, 4 * C], "bfloat16"),
+    "ztu": ("sbuf", [128, 4 * H], "bfloat16"), "ztl": ("sbuf", [128, 4 * H], "bfloat16"),
+    "yt": ("sbuf", [128, C], "float32"), "g2": ("sbuf", [128, 4 * C], "bfloat16"),
+}
+for k in range(8):
+    SCRATCH["b%d" % k] = ("psum", [128, 512], "float32")
+for k in range(4):
+    SCRATCH["xq%d" % k] = ("sbuf", [128, C], "float8_e4m3fn_x4")
+    SCRATCH["xs%d" % k] = ("sbuf", [128, C], "uint8")
+for k in range(3):
+    for nm in ("zu", "zl", "zr"):
+        SCRATCH["%sq%d" % (nm, k)] = ("sbuf", [128, H], "float8_e4m3fn_x4")
+        SCRATCH["%ss%d" % (nm, k)] = ("sbuf", [128, H], "uint8")
+    SCRATCH["oc%d" % k] = ("sbuf", [128, 44], "uint16")
+    SCRATCH["f16%d" % k] = ("sbuf", [128, 22], "uint16")
+    SCRATCH["fs%d" % k] = ("sbuf", [128, 22], "uint16")
+    SCRATCH["sel%d" % k] = ("sbuf", [128, 66], "float32")
+    SCRATCH["ba%d" % k] = ("sbuf", [128, 66], "float32")
+    SCRATCH["di%d" % k] = ("sbuf", [128, 66], "float32")
+    SCRATCH["rep%d" % k] = ("sbuf", [128, 2 * C], "float32")
+SCRATCH["fia"] = ("sbuf", [128, 66], "int32")
+SCRATCH["pka"] = ("sbuf", [128, 66], "uint16")
+SCRATCH["e16a"] = ("sbuf", [128, 66], "uint16")
+SCRATCH["fua"] = ("sbuf", [128, 36], "uint16")
+SCRATCH["mra"] = ("sbuf", [128, 3 * C], "float32")
+SCRATCH["rep3"] = ("sbuf", [128, 2 * C], "float32")
+SCRATCH["hq"] = ("sbuf", [128, H // 2], "float8_e4m3fn_x4")
+SCRATCH["hs"] = ("sbuf", [128, H // 2], "uint8")
+SCRATCH["hl"] = ("sbuf", [128, 22], "uint16")
+
+ENG = {"V": "sv", "S": "ss", "P": "st", "G": "sg"}
+SEMAPHORES = ["sv", "ss", "st", "sg", "rl", "hla", "hca", "hsa"] + ["la%d" % k for k in range(3)] + ["za%d" % k for k in range(3)] + ["d%d" % k for k in range(40)]
+
+
+def machine(g, T):
+    queues = {"V": g.vector, "S": g.scalar, "P": g.tensor, "G": g, "Y": g.sync}
+    know = {q: {} for q in queues}
+    cnt, hist, behind, ndma = {}, {}, {}, [0]
+
+    def need(q, tok):
+        sem, val = tok
+        k = know[q]
+        if k.get(sem, 0) >= val:
+            return
+        queues[q].wait_ge(T.sem[sem], val)
+        k[sem] = val
+        for s, v in behind.get(tok, {}).items():
+            k[s] = max(k.get(s, 0), v)
+
+    def norm(rs):
+        return [(r, 0, 1 << 30) if isinstance(r, str) else r for r in rs]
+
+    def before(q, rd, wr):
+        toks = []
+        for key, lo, hi in rd:
+            toks += [tok for (l, h, tok, w) in hist.get(key, []) if w and l < hi and lo < h]
+        for key, lo, hi in wr:
+            toks += [tok for (l, h, tok, w) in hist.get(key, []) if l < hi and lo < h]
+        best = {}
+        for s, v in toks:
+            best[s] = max(best.get(s, 0), v)
+        own = ENG.get(q)
+        for s in sorted(best, key=lambda s: s == own):
+            need(q, (s, best[s]))
+
+    def after(tok, rd, wr):
+        for key, lo, hi in wr:
+            hist[key] = [e for e in hist.get(key, []) if not (lo <= e[0] and e[1] <= hi)] + [(lo, hi, tok, True)]
+        for key, lo, hi in rd:
+            hist.setdefault(key, []).append((lo, hi, tok, False))
+
+    def op(q, call, rd, wr):
+        rd, wr = norm(rd), norm(wr)
+        before(q, rd, wr)
+        sem = ENG[q]
+        cnt[sem] = cnt.get(sem, 0) + 1
+        tok = (sem, cnt[sem])
+        call(queues[q]).then_inc(T.sem[sem], 1)
+        behind[tok] = dict(know[q])
+        after(tok, rd, wr)
+
+    def dma(q, out, in_, rd, wr):
+        rd, wr = norm(rd), norm(wr)
+        before(q, rd, wr)
+        sem = "d%d" % ndma[0]
+        ndma[0] += 1
+        cnt[sem] = 16
+        queues[q].dma_start(out, in_).then_inc(T.sem[sem], 16)
+        behind[(sem, 16)] = dict(know[q])
+        after((sem, 16), rd, wr)
+
+    def lands(key, sem, val):
+        after((sem, val), [], norm([key]))
+
+    def sends(rd, n, call):
+        before("G", norm(rd), [])
+        call()
+        cnt["rl"] = cnt.get("rl", 0) + n
+
+    def finish():
+        for s in sorted(cnt, key=lambda s: s[0] == "d"):
+            need("Y", (s, cnt[s]))
+    return op, dma, lands, sends, finish
+
+
+def bits(topo, src, dst, n=16, skip=0):
+    e = topo.engines(src, dst)[skip:skip + n]
+    return sum(1 << i for i in e), len(e)
+
+
+def helpers(T, topo, src, dst):
+    if topo.may_write(src, dst):
+        return []
+    return [c for c in topo.cores_of(src) if c not in T.cores and topo.die(c) == topo.die(src) and topo.may_write(c, dst)][:2]
+
+
+def send(g, T, topo, src, dst, out, in_, rsem, n=16):
+    rid, pid = topo.addr(dst, src)
+    m, k = bits(topo, src, dst, n)
+    g.remote_dma(out_ap=out, in_ap=in_, remote_sem=T.sem[rsem], local_sem=T.sem.rl, pid=pid, routing_id=rid, dma_engine_mask=m)
+    return k
+
+
+def hand_on(g, core, T, topo):
+    n = [0]
+    for r, src in enumerate(T.cores):
+        for s in STEP:
+            dst = T.cores[r ^ s]
+            hp = helpers(T, topo, src, dst)
+            if core not in hp:
+                continue
+            h, t = hp.index(core), STEP.index(s)
+            lo, hi = h * H // 2, (h + 1) * H // 2
+            if h == len(hp) - 1:
+                g.wait_ge(T.sem.hla, bits(topo, src, core)[1])
+                n[0] += send(g, T, topo, core, dst, T["fs%d" % t][:, 0:22], T.hl[:, 0:22], "la%d" % t)
+            g.wait_ge(T.sem.hca, 8)
+            n[0] += send(g, T, topo, core, dst, T["zrq%d" % t][:, lo:hi].bitcast(dt.uint8), T.hq[:, 0:H // 2].bitcast(dt.uint8), "za%d" % t)
+            g.wait_ge(T.sem.hsa, 8)
+            n[0] += send(g, T, topo, core, dst, T["zrs%d" % t][:, lo:hi], T.hs[:, 0:H // 2], "za%d" % t)
+    if n[0]:
+        g.wait_ge(T.sem.rl, n[0])
+
+
+def rank_program(g, core, T, topo):
+    rank = T.rank_of(core)
+    if rank is None:
+        return hand_on(g, core, T, topo)
+    op, dma, lands, sends, finish = machine(g, T)
+    copy, sign = F.Copy, F.Sign
+
+    for t in range(3):
+        src = T.cores[rank ^ STEP[t]]
+        hp = helpers(T, topo, src, core)
+        if hp:
+            lands("fs%d" % t, "la%d" % t, bits(topo, hp[-1], core)[1])
+            lands("zr%d" % t, "za%d" % t, sum(2 * bits(topo, h, core)[1] for h in hp))
+        else:
+            lands("fs%d" % t, "la%d" % t, bits(topo, src, core)[1])
+            lands("zr%d" % t, "za%d" % t, 2 * bits(topo, src, core)[1])
+
+    for i, (a, b) in enumerate(CH):
+        dma("Y", T.xin[:, 4 * a:4 * b], T.x[:, 4 * a:4 * b], [], ["xin%d" % i])
+    dma("S", T.ppi[:, :], T.pp[:, :], [], ["ppi"])
+    dma("S", T.pri[:, :], T.pr[:, :], [], ["pri"])
+    dma("S", T.ut[:, :], T.u[:, :], [], ["ut"])
+    dma("S", T.rfi[:, :], T.rf[:, :], [], ["rfi"])
+    dma("Y", T.wq[:, 0:512].bitcast(dt.uint8), T.wc[:, :], [], ["wq"])
+    dma("Y", T.wsp[:, 0:512], T.ws[:, :], [], ["wsp"])
+    dma("Y", T.vt[:, :], T.v[:, :], [], ["vt"])
+
+    op("V", lambda q: q.memset(T.one[:, :], 1.0), [], ["one"])
+    op("V", lambda q: q.memset(T.bw[:, 352:512], 0.0), [], [("bw", 352, 512)])
+    op("G", lambda q: q.iota(T.jj[:, :], [[0, 22], [1, 16]], 128, -1), [], ["jj"])
+    op("G", lambda q: q.iota(T.idx[:, :], [[1, C]], 0, 0, allow_small_or_imprecise_dtypes=True), [], ["idx"])
+    op("G", lambda q: q.iota(T.uoi[:, :], [[1, 2], [16, 8]], 0, 0), [], ["uoi"])
+    op("G", lambda q: q.iota(T.pm[:, :], [[0, 66]], 0, 1), [], ["pm"])
+    op("G", lambda q: q.iota(T.q16[:, :], [[0, 3], [16, 22]], 352, 0), [], ["q16"])
+    op("G", lambda q: q.iota(T.j16[:, :], [[0, 22], [1, 16]], 0, 0), [], ["j16"])
+    op("G", lambda q: q.affine_select(T.et[:, :], T.one[:, :], [[1, 4], [-4, 128], [-1, 4]], A.is_equal, 0.0, 0, 4), ["one"], ["et"])
+    op("V", lambda q: q.tensor_scalar(T.dd[:, :], T.jj[:, :], 15, None, A.bitwise_and), ["jj"], ["dd"])
+    op("V", lambda q: q.tensor_scalar(T.c1[:, :], T.dd[:, :], 1.0, BIG - 1.0, A.is_equal, A.mult), ["dd"], ["c1"])
+    op("V", lambda q: q.tensor_scalar(T.ck[:, :], T.dd[:, :], 0.0, None, A.is_gt), ["dd"], ["ck"])
+    op("V", lambda q: q.tensor_scalar(T.wt[:, 1:2], T.dd[:, 15:16], 0.0, 1.0 - 1.0 / BIG, A.is_equal, A.mult), ["dd"], ["wt1"])
+    op("V", lambda q: q.tensor_copy(T.uo[:, :], T.uoi[:, :]), ["uoi"], ["uo"])
+    op("V", lambda q: q.tensor_tensor(T.ck[:, :], T.c1[:, :], T.ck[:, :], A.add), ["c1", "ck"], ["ck"])
+    op("V", lambda q: q.tensor_scalar(T.wt[:, 0:1], T.wt[:, 1:2], 1.0 / BIG, None, A.add), ["wt1"], ["wt0"])
+
+    op("V", lambda q: q.tensor_copy(T.pp16[:, :], T.ppi[:, :]), ["ppi"], ["pp16"])
+    op("V", lambda q: q.tensor_copy(T.pr16[:, :], T.pri[:, :]), ["pri"], ["pr16"])
+    op("S", lambda q: q.activation(T.rep0[:, 0:C], T.idx[:, :].indirect(T.pp16[:, 0:22]), copy), ["pp16", "idx"], [("rep0", 0, C)])
+    op("V", lambda q: q.tensor_copy(T.rf16[:, :], T.rfi[:, :]), ["rfi"], ["rf16"])
+    op("V", lambda q: q.tensor_copy(T.rep0[:, C:2 * C], T.idx[:, :].indirect(T.rf16[:, 0:22])), ["rf16", "idx"], [("rep0", C, 2 * C)])
+
+    def quant(t, i, buf, keys):
+        a, b = CH[i]
+        op("V", lambda q: q.quantize_mx(T["xq%d" % t][:, a:b], T["xs%d" % t][:, a:b], T[buf][:, 4 * a:4 * b]), keys, [("xq%d" % t, a, b)])
+
+    op("V", lambda q: q.quantize_mx(T.uq[:, :], T.us[:, :], T.ut[:, :]), ["ut"], ["uq"])
+    op("V", lambda q: q.tensor_copy(T.ua[:, 0:256].bitcast(dt.uint32), T.uq[:, 0:128].bitcast(dt.uint32).indirect(T.uo[:, 0:16])), ["uq", "uo"], ["ua"])
+    op("V", lambda q: q.tensor_copy(T.uas[:, 0:256], T.us[:, 0:128].indirect(T.uo[:, 0:16])), ["uq", "uo"], ["uas"])
+
+    def mm(bank, side, scale, c0, rq, rs, a, b, rd):
+        op("P", lambda q: q.matmul_mx(T["b%d" % bank][:, 0:b - a], T[side][:, c0:c0 + 128], T[scale][:, c0:c0 + 128],
+                                      T[rq][:, a:b], T[rs][:, a:b], True, True), rd, ["b%d" % bank])
+
+    def unpack(t, p, a, b):
+        mm(4 + p, "eq", "es", 128 * p, "xq%d" % t, "xs%d" % t, a, b, ["eq", ("xq%d" % t, a, b)])
+
+    def evac(p, a, b):
+        op("S", lambda q: q.activation(T.fp[:, C * p + a:C * p + b], T["b%d" % (4 + p)][:, 0:b - a], copy), [], ["b%d" % (4 + p), ("fp%d" % p, a, b)])
+
+    def signs(t, i):
+        a, b = CH[i]
+        for n in range(2):
+            mm(2 * i + n, "ua", "uas", 128 * n, "xq%d" % t, "xs%d" % t, a, b, ["ua", "uas", ("xq%d" % t, a, b)])
+        tiny = -(2.0 ** -100)
+        op("S", lambda q: q.activation(T.sa[:, a:b], T["b%d" % (2 * i)][:, 0:b - a], sign, bias=tiny), [], ["b%d" % (2 * i), ("sa", a, b)])
+        op("S", lambda q: q.activation(T.bw[:, a:b], T["b%d" % (2 * i + 1)][:, 0:b - a], sign, bias=tiny), [], ["b%d" % (2 * i + 1), ("bw", a, b)])
+
+    def head(t, i):
+        signs(t, i)
+        if i == 0:
+            for p in (0, 1):
+                unpack(t, p, *CH[0])
+                evac(p, *CH[0])
+        else:
+            for p in (2, 3):
+                unpack(t, p, 0, C)
+                evac(p, 0, C)
+            for p in (0, 1):
+                unpack(t, p, *CH[1])
+                evac(p, *CH[1])
+
+    def compose(t, rep):
+        k = T.pr16[:, 22 * t:22 * t + 22]
+        op("S", lambda q: q.activation(T.pkf[:, 0:C], T[rep][:, 0:C].indirect(k), copy), ["pr16", (rep, 0, C)], [("pkf", 0, C)])
+        op("S", lambda q: q.activation(T.pkf[:, C:2 * C], T[rep][:, C:2 * C].indirect(k), copy), ["pr16", (rep, C, 2 * C)], [("pkf", C, 2 * C)])
+
+    def kplus(t, q0):
+        k = T.pr16[:, 22 * t:22 * t + 22]
+        if q0 == "V":
+            op("V", lambda q: q.tensor_scalar(T.mra[:, C * t:C * t + C], T.idx[:, :].indirect(k), 1024.0, None, A.add), ["pr16", "idx"], ["mr%d" % t])
+        else:
+            op("S", lambda q: q.activation(T.mra[:, C * t:C * t + C], T.idx[:, :].indirect(k), F.Identity, bias=1024.0), ["pr16", "idx"], ["mr%d" % t])
+
+    def scan(out, okey, lo, fac, data, dkey):
+        op("V", lambda q: q.tensor_tensor_scan(T[out][:, lo:lo + C], T[fac][:, :], data, 0.0, A.mult, A.add), [fac, dkey], [(okey, lo, lo + C)])
+
+    def finish_lists(t, psrc, pkey, fsrc, fkey):
+        ba, di = "ba%d" % t, "di%d" % t
+        for n, (s, key) in enumerate(((psrc, pkey), (fsrc, fkey), (fsrc, fkey))):
+            op("V", lambda q: q.tensor_copy(T[ba][:, 22 * n:22 * n + 22], s), [key], [(ba, 22 * n, 22 * n + 22)])
+        scan("sp", "sp", 0, "ck", T.pkf[:, 0:C], ("pkf", 0, C))
+        scan("sp", "sp", C, "ck", T.pkf[:, C:2 * C], ("pkf", C, 2 * C))
+        op("V", lambda q: q.tensor_scalar(T.x1[:, 0:44], T.sp[:, 15:2 * C:16], T.wt[:, 0:1], None, A.mult), ["sp", "wt0"], [("x1", 0, 44)])
+        op("V", lambda q: q.tensor_copy(T.pka[:, 22 * t:22 * t + 22], T.x1[:, 0:22]), [("x1", 0, 22)], ["pk16%d" % t])
+        op("V", lambda q: q.tensor_tensor(T.xx[:, :], T.x1[:, 22:44], T.qk[:, 22 * t:22 * t + 22], A.add), [("x1", 22, 44), "qk"], ["xx"])
+        op("V", lambda q: q.tensor_scalar(T.nn[:, :], T.xx[:, :], 1.0 / 352, 0.4986, A.mult, A.subtract), ["xx"], ["nn"])
+        op("V", lambda q: q.tensor_scalar(T.nn[:, :], T.nn[:, :], -352.0, None, A.mult), ["nn"], ["nn"])
+        op("V", lambda q: q.tensor_tensor(T.x1[:, 44:66], T.xx[:, :], T.nn[:, :], A.add), ["xx", "nn"], [("x1", 44, 66)])
+        op("V", lambda q: q.tensor_tensor(T[di][:, :], T.x1[:, :], T[ba][:, :], A.subtract), ["x1", ba], [di])
+        op("V", lambda q: q.tensor_scalar(T[ba][:, 22:44], T[ba][:, 22:44], 512.0, None, A.add), [(ba, 22, 44)], [(ba, 22, 44)])
+
+    kplus(0, "V")
+    compose(0, "rep0")
+    quant(0, 0, "xin", ["xin0"])
+    op("V", lambda q: q.quantize_mx(T.eq[:, :], T.es[:, :], T.et[:, :]), ["et"], ["eq"])
+    quant(0, 1, "xin", ["xin1"])
+    head(0, 0)
+    head(0, 1)
+    op("V", lambda q: q.tensor_scalar(T.pm[:, :], T.pm[:, :], 15, None, A.bitwise_and), ["pm"], ["pm"])
+    op("V", lambda q: q.tensor_tensor(T.qq[:, :], T.pm[:, :], T.q16[:, :], A.add), ["pm", "q16"], ["qq"])
+    op("V", lambda q: q.tensor_tensor(T.qk[:, :], T.qq[:, :], T.pri[:, :], A.subtract), ["qq", "pri"], ["qk"])
+    finish_lists(0, T.ppi[:, :], "ppi", T.rfi[:, :], "rfi")
+    op("V", lambda q: q.tensor_scalar(T.mk[:, 0:C], T.dd[:, :], 0.0, 4096.0, A.is_equal, A.mult), ["dd"], [("mk", 0, C)])
+    op("V", lambda q: q.tensor_scalar(T.mk[:, C:2 * C], T.dd[:, :], 0.0, None, A.is_equal), ["dd"], [("mk", C, 2 * C)])
+    op("V", lambda q: q.tensor_scalar(T.c01[:, :], T.j16[:, :], 1.0, None, A.min), ["j16"], ["c01"])
+
+    p16, p16key = T.pp16[:, 0:22], "pp16"
+    for t in range(3):
+        fi_, fu_, e_ = T.fia[:, 22 * t:22 * t + 22], T.fua[:, 12 * t:12 * t + 11], T.e16a[:, 22 * t:22 * t + 22]
+        ba, di, oc, sel, f16, fu, fi = [n + str(t) for n in ("ba", "di", "oc", "sel", "f16", "fu", "fi")]
+        op("V", lambda q: q.tensor_tensor(T.am[:, :], T.sa[:, :].indirect(p16), T.mra[:, C * t:C * t + C], A.mult), ["sa", p16key, "mr%d" % t], ["am"])
+        op("V", lambda q: q.tensor_tensor(T.bw[:, 512:864], T.sa[:, :].indirect(T.pka[:, 22 * t:22 * t + 22]), T.am[:, :], A.mult), ["sa", "pk16%d" % t, "am"], [("bw", 512, 864)])
+        scan("sE", "sE", 0, "ck", T.bw[:, 512:864], ("bw", 512, 864))
+
+        def eqs(n):
+            op("V", lambda q: q.tensor_scalar(T.e3[:, 22 * n:22 * n + 22], T.sE[:, 15:C:16], 0.0, None, A.is_gt), ["sE"], [("e3", 22 * n, 22 * n + 22)])
+
+        def choose(a, b):
+            op("V", lambda q: q.tensor_tensor(T.sm[:, a:b], T.e3[:, a:b], T[di][:, a:b], A.mult), [("e3", a, b), di], [("sm", a, b)])
+            op("V", lambda q: q.tensor_tensor(T[sel][:, a:b], T.sm[:, a:b], T[ba][:, a:b], A.add), [("sm", a, b), ba], [(sel, a, b)])
+        eqs(0)
+        eqs(1)
+        choose(0, 44)
+        op("V", lambda q: q.tensor_copy(T[oc][:, :], T[sel][:, 0:44]), [(sel, 0, 44)], [oc])
+        for p in range(4):
+            op("S", lambda q: q.activation(T.gp[:, C * p:C * p + C], T.fp[:, C * p:C * p + C].indirect(T[oc][:, 0:22]), copy, scale=0.5), ["fp%d" % p, oc], ["gp%d" % p])
+        op("V", lambda q: q.tensor_tensor(T.gm[:, :], T.bw[:, :].indirect(T[oc][:, 0:44]), T.mk[:, :], A.mult), ["bw", oc, "mk"], ["gm"])
+        eqs(2)
+        choose(44, 66)
+        scan("gs", "gs", 0, "c01", T.gm[:, 0:C], "gm")
+        scan("gs", "gs", C, "c01", T.gm[:, C:2 * C], "gm")
+        op("V", lambda q: q.tensor_tensor(T.tt[:, 0:22], T.gs[:, C + 15:2 * C:16], T[sel][:, 22:44], A.max), ["gs", sel], ["t1"])
+        op("V", lambda q: q.tensor_tensor(T.tt[:, 22:44], T.gs[:, 15:C:16], T.tt[:, 0:22], A.min), ["gs", "t1"], ["t2"])
+        op("V", lambda q: q.tensor_tensor(T.t3[:, :], T.tt[:, 22:44], T[sel][:, 44:66], A.max), ["t2", sel], ["t3"])
+        op("V", lambda q: q.tensor_scalar(fi_, T.t3[:, :], 511, None, A.bitwise_and), ["t3"], [fi])
+        op("V", lambda q: q.tensor_copy(fu_, T.fia[:, 22 * t + 11:22 * t + 22]), [fi], [fu])
+        op("V", lambda q: q.tensor_copy(T[f16][:, :], fi_), [fi], [f16])
+        dst = T.cores[rank ^ STEP[t]]
+        hp = helpers(T, topo, core, dst)
+        far = hp[-1] if hp else dst
+        sends([f16], bits(topo, core, far)[1], lambda: send(g, T, topo, core, far, T.hl[:, 0:22] if hp else T["fs%d" % t][:, 0:22], T[f16][:, 0:22], "hla" if hp else "la%d" % t))
+        for half, (buf, off, o, nm) in enumerate((("ztu", fu_, H, "zu"), ("ztl", T[f16][:, 0:11], 0, "zl"))):
+            zq, zs = "%sq%d" % (nm, t), "%ss%d" % (nm, t)
+            for p in range(4):
+                a, b = C * p + o, C * p + o + H
+                if half == 0:
+                    op("V", lambda q: q.tensor_copy(T.g2[:, a:b], T.gp[:, a:b]), ["gp%d" % p], [("g2", a, b)])
+                else:
+                    op("S", lambda q: q.activation(T.g2[:, a:b], T.gp[:, a:b], copy), ["gp%d" % p], [("g2", a, b)])
+            for p in range(4):
+                a, b = C * p + o, C * p + o + H
+                op("V", lambda q: q.tensor_tensor(T[buf][:, p:4 * H:4], T.gp[:, C * p:C * p + C].indirect(off), T.g2[:, a:b], A.add), ["gp%d" % p, ("g2", a, b), f16, fu], ["%s_%d" % (buf, p)])
+            op("V", lambda q: q.quantize_mx(T[zq][:, :], T[zs][:, :], T[buf][:, :]), ["%s_%d" % (buf, p) for p in range(4)], [zq])
+            if half == 0 and not hp:
+                k = bits(topo, core, dst)[1]
+                sends([zq], k, lambda: send(g, T, topo, core, dst, T["zrq%d" % t][:, 0:H].bitcast(dt.uint8), T[zq][:, 0:H].bitcast(dt.uint8), "za%d" % t))
+                sends([zq], k, lambda: send(g, T, topo, core, dst, T["zrs%d" % t][:, 0:H], T[zs][:, 0:H], "za%d" % t))
+            elif half == 0:
+                cd, sc = [], []
+                for h, c in enumerate(hp):
+                    rid, pid = topo.addr(c, core)
+                    m = bits(topo, core, c, 8, 8 * h)[0]
+                    lo, hi = h * H // 2, (h + 1) * H // 2
+                    cd.append(RemoteDMATransfer(dst_ids=[DstId(rid=rid, pnc=pid)], dma_engine_mask=m, remote_sem=T.sem.hca, src=T[zq][:, lo:hi].bitcast(dt.uint8), dst=T.hq[:, 0:H // 2].bitcast(dt.uint8)))
+                    sc.append(RemoteDMATransfer(dst_ids=[DstId(rid=rid, pnc=pid)], dma_engine_mask=m, remote_sem=T.sem.hsa, src=T[zs][:, lo:hi], dst=T.hs[:, 0:H // 2]))
+                sends([zq], 8 * len(hp), lambda: g.remote_dma_fused(cd, local_sem=T.sem.rl))
+                sends([zq], 8 * len(hp), lambda: g.remote_dma_fused(sc, local_sem=T.sem.rl))
+        rep = "rep%d" % (t + 1)
+        op("S", lambda q: q.activation(T[rep][:, 0:C], T.idx[:, :].indirect(T[oc][:, 0:22]), copy), [oc, "idx"], [(rep, 0, C)])
+        op("S", lambda q: q.activation(T[rep][:, C:2 * C], T.idx[:, :].indirect(T[f16][:, 0:22]), copy), [f16, "idx"], [(rep, C, 2 * C)])
+        for p in range(4):
+            mm(4 + p, "wq", "wsp", 128 * p, "zlq%d" % t, "zls%d" % t, 0, H, ["wq", "wsp", "zlq%d" % t])
+        op("S", lambda q: q.activation(T.fsr[:, :], T.idx[:, :].indirect(T["fs%d" % t][:, 0:22]), copy), ["fs%d" % t, "idx"], ["fsr"])
+        op("S", lambda q: q.activation(T.hr[:, :], T.fsr[:, :].indirect(T[f16][:, 0:22]), copy), ["fsr", f16], ["hr"])
+        for p in range(4):
+            op("S", lambda q: q.activation(T.bp[:, C * p:C * p + H], T["b%d" % (4 + p)][:, 0:H], copy, scale=0.03125), [], ["b%d" % (4 + p), ("bp%d" % p, 0, H)])
+        op("V", lambda q: q.tensor_copy(T.ew[:, :].indirect(T[oc][:, 0:22]), T.hr[:, :]), ["hr", oc], ["ew"])
+        scan("esc", "esc", 0, "ck", T.ew[:, :], "ew")
+        op("V", lambda q: q.tensor_scalar(T.ei[:, :], T.esc[:, 15:C:16], T.wt[:, 0:1], None, A.mult), ["esc", "wt0"], ["ei"])
+        op("V", lambda q: q.tensor_copy(e_, T.ei[:, :]), ["ei"], ["e16%d" % t])
+
+        def next_lists():
+            finish_lists(t + 1, T[sel][:, 0:22], (sel, 0, 22), fi_, fi)
+        if t < 2 and not LATE[t]:
+            kplus(t + 1, "S")
+            compose(t + 1, rep)
+            next_lists()
+        if t == 0:
+            op("V", lambda q: q.quantize_mx(T.vq[:, :], T.vs[:, :], T.vt[:, :]), ["vt"], ["vq"])
+        if t == 2:
+            dma("Y", T.pf[:, :], T[rep][0:128:16, :], [rep], ["pf"])
+        for p in range(4):
+            mm(p, "wq", "wsp", 128 * p, "zrq%d" % t, "zrs%d" % t, 0, H, ["wq", "wsp", "zr%d" % t])
+            o, i_ = T.bp[:, C * p + H:C * p + C], T["b%d" % p][:, 0:H]
+            if p % 2 == 0:
+                op("S", lambda q: q.activation(o, i_, copy, scale=0.03125), [], ["b%d" % p, ("bp%d" % p, H, C)])
+            else:
+                op("V", lambda q: q.tensor_scalar(o, i_, 0.03125, None, A.mult), [], ["b%d" % p, ("bp%d" % p, H, C)])
+        if t < 2 and LATE[t]:
+            kplus(t + 1, "S")
+            compose(t + 1, rep)
+        for i, (a, b) in enumerate(CH):
+            for p in range(4):
+                op("V", lambda q: q.tensor_tensor(T.xt[:, 4 * a + p:4 * b:4], T.bp[:, C * p:C * p + C].indirect(T.e16a[:, 22 * t + a // 16:22 * t + b // 16]), T.fp[:, C * p + a:C * p + b], A.add),
+                   ["bp%d" % p, "e16%d" % t, ("fp%d" % p, a, b)], [("xt%d" % p, a, b)])
+            quant(t + 1, i, "xt", [("xt%d" % p, a, b) for p in range(4)])
+            if t < 2:
+                head(t + 1, i)
+            else:
+                xq, xs = "xq%d" % 3, "xs%d" % 3
+                mm(4 + i, "vq", "vs", 0, xq, xs, a, b, ["vq", (xq, a, b)])
+                dma("Y", T.oc[:, 4 * a:4 * b], T[xq][:, a:b].bitcast(dt.uint8), [(xq, a, b)], ["ocout%d" % i])
+                op("S", lambda q: q.activation(T.yt[:, a:b], T["b%d" % (4 + i)][:, 0:b - a], copy), [], ["b%d" % (4 + i), ("yt", a, b)])
+                dma("S", T.y[:, a:b], T.yt[:, a:b], [("yt", a, b)], ["yout%d" % i])
+                for k in range(4):
+                    dma("Y" if k < 3 else "S", T.osc[4 * k:4 * k + 4, a:b], T[xs][32 * k:32 * k + 4, a:b], [(xq, a, b)], ["oscout%d%d" % (i, k)])
+        if t < 2 and LATE[t]:
+            next_lists()
+        p16, p16key = T[oc][:, 0:22], oc
+    finish()

@@ -1,11 +1,10 @@
-from concourse.bass import DstId, RemoteDMATransfer
 from concourse.mybir import dt, AluOpType, ActivationFunctionType
 
 A, F = AluOpType, ActivationFunctionType
 N, C, H = 8, 352, 176
 STEP = [4, 1, 2]
 CH = [(0, 224), (224, 352)]
-LATE = [False, True]
+XS = [2, 2, 2]
 BIG = 16384.0
 
 SCRATCH = {
@@ -15,15 +14,15 @@ SCRATCH = {
     "ua": ("sbuf", [128, 256], "float8_e4m3fn_x4"), "uas": ("sbuf", [128, 256], "uint8"),
     "vq": ("sbuf", [128, 128], "float8_e4m3fn_x4"), "vs": ("sbuf", [128, 128], "uint8"),
     "wq": ("sbuf", [128, 512], "float8_e4m3fn_x4"), "wsp": ("sbuf", [128, 512], "uint8"),
-    "one": ("sbuf", [128, 2048], "bfloat16"), "et": ("sbuf", [128, 2048], "bfloat16"),
+    "one": ("sbuf", [128, 128], "bfloat16"), "gb": ("sbuf", [128, C], "bfloat16"), "gsb": ("sbuf", [128, C], "bfloat16"), "c0b": ("sbuf", [128, C], "bfloat16"),
+    "bg": ("sbuf", [128, 4 * C], "bfloat16"), "et": ("sbuf", [128, 2048], "bfloat16"),
     "eq": ("sbuf", [128, 512], "float8_e4m3fn_x4"), "es": ("sbuf", [128, 512], "uint8"),
     "ppi": ("sbuf", [128, 22], "int32"), "rfi": ("sbuf", [128, 22], "int32"), "pri": ("sbuf", [128, 66], "int32"),
     "pp16": ("sbuf", [128, 22], "uint16"), "rf16": ("sbuf", [128, 22], "uint16"), "pr16": ("sbuf", [128, 66], "uint16"),
-    "idx": ("sbuf", [128, C], "float32"), "jj": ("sbuf", [128, C], "int32"), "dd": ("sbuf", [128, C], "int32"),
-    "mk": ("sbuf", [128, 2 * C], "float32"), "c1": ("sbuf", [128, C], "float32"),
-    "ck": ("sbuf", [128, C], "float32"), "j16": ("sbuf", [128, C], "int32"), "c01": ("sbuf", [128, C], "float32"),
-    "wt": ("sbuf", [128, 2], "float32"), "uoi": ("sbuf", [128, 16], "int32"), "uo": ("sbuf", [128, 16], "uint16"),
-    "pm": ("sbuf", [128, 66], "int32"), "q16": ("sbuf", [128, 66], "int32"),
+    "idx": ("sbuf", [128, C], "float32"), "jm": ("sbuf", [128, C], "float32"), "mk": ("sbuf", [128, 2 * C], "float32"),
+    "ck": ("sbuf", [128, C], "float32"), "c01": ("sbuf", [128, C], "float32"),
+    "wt": ("sbuf", [128, 8], "float32"), "uo": ("sbuf", [128, 16], "uint16"),
+    "pm": ("sbuf", [128, 66], "int32"), "q16": ("sbuf", [128, 82], "int32"),
     "qq": ("sbuf", [128, 66], "int32"), "qk": ("sbuf", [128, 66], "float32"),
     "sa": ("sbuf", [128, C], "bfloat16"), "bw": ("sbuf", [128, 864], "float32"), "am": ("sbuf", [128, C], "float32"),
     "sE": ("sbuf", [128, C], "float32"), "e3": ("sbuf", [128, 66], "float32"), "sm": ("sbuf", [128, 66], "float32"),
@@ -59,8 +58,8 @@ SCRATCH["e16a"] = ("sbuf", [128, 66], "uint16")
 SCRATCH["fua"] = ("sbuf", [128, 36], "uint16")
 SCRATCH["mra"] = ("sbuf", [128, 3 * C], "float32")
 SCRATCH["rep3"] = ("sbuf", [128, 2 * C], "float32")
-SCRATCH["hq"] = ("sbuf", [128, H // 2], "float8_e4m3fn_x4")
-SCRATCH["hs"] = ("sbuf", [128, H // 2], "uint8")
+SCRATCH["hq"] = ("sbuf", [128, H], "float8_e4m3fn_x4")
+SCRATCH["hs"] = ("sbuf", [128, H], "uint8")
 SCRATCH["hl"] = ("sbuf", [128, 22], "uint16")
 
 ENG = {"V": "sv", "S": "ss", "P": "st", "G": "sg"}
@@ -164,15 +163,16 @@ def hand_on(g, core, T, topo):
             hp = helpers(T, topo, src, dst)
             if core not in hp:
                 continue
-            h, t = hp.index(core), STEP.index(s)
-            lo, hi = h * H // 2, (h + 1) * H // 2
-            if h == len(hp) - 1:
-                g.wait_ge(T.sem.hla, bits(topo, src, core)[1])
+            t, k = STEP.index(s), bits(topo, src, core)[1]
+            if core == hp[-1]:
+                g.wait_ge(T.sem.hla, k)
                 n[0] += send(g, T, topo, core, dst, T["fs%d" % t][:, 0:22], T.hl[:, 0:22], "la%d" % t)
-            g.wait_ge(T.sem.hca, 8)
-            n[0] += send(g, T, topo, core, dst, T["zrq%d" % t][:, lo:hi].bitcast(dt.uint8), T.hq[:, 0:H // 2].bitcast(dt.uint8), "za%d" % t)
-            g.wait_ge(T.sem.hsa, 8)
-            n[0] += send(g, T, topo, core, dst, T["zrs%d" % t][:, lo:hi], T.hs[:, 0:H // 2], "za%d" % t)
+            if core == hp[0]:
+                g.wait_ge(T.sem.hca, k)
+                n[0] += send(g, T, topo, core, dst, T["zrq%d" % t][:, 0:H].bitcast(dt.uint8), T.hq[:, 0:H].bitcast(dt.uint8), "za%d" % t)
+            if core == hp[-1]:
+                g.wait_ge(T.sem.hsa, k)
+                n[0] += send(g, T, topo, core, dst, T["zrs%d" % t][:, 0:H], T.hs[:, 0:H], "za%d" % t)
     if n[0]:
         g.wait_ge(T.sem.rl, n[0])
 
@@ -189,7 +189,7 @@ def rank_program(g, core, T, topo):
         hp = helpers(T, topo, src, core)
         if hp:
             lands("fs%d" % t, "la%d" % t, bits(topo, hp[-1], core)[1])
-            lands("zr%d" % t, "za%d" % t, sum(2 * bits(topo, h, core)[1] for h in hp))
+            lands("zr%d" % t, "za%d" % t, bits(topo, hp[0], core)[1] + bits(topo, hp[-1], core)[1])
         else:
             lands("fs%d" % t, "la%d" % t, bits(topo, src, core)[1])
             lands("zr%d" % t, "za%d" % t, 2 * bits(topo, src, core)[1])
@@ -205,35 +205,36 @@ def rank_program(g, core, T, topo):
     dma("Y", T.vt[:, :], T.v[:, :], [], ["vt"])
 
     op("V", lambda q: q.memset(T.one[:, :], 1.0), [], ["one"])
+    op("V", lambda q: q.memset(T.et[:, :], 0.0), [], ["et"])
     op("V", lambda q: q.memset(T.bw[:, 352:512], 0.0), [], [("bw", 352, 512)])
-    op("G", lambda q: q.iota(T.jj[:, :], [[0, 22], [1, 16]], 128, -1), [], ["jj"])
-    op("G", lambda q: q.iota(T.idx[:, :], [[1, C]], 0, 0, allow_small_or_imprecise_dtypes=True), [], ["idx"])
-    op("G", lambda q: q.iota(T.uoi[:, :], [[1, 2], [16, 8]], 0, 0), [], ["uoi"])
     op("G", lambda q: q.iota(T.pm[:, :], [[0, 66]], 0, 1), [], ["pm"])
-    op("G", lambda q: q.iota(T.q16[:, :], [[0, 3], [16, 22]], 352, 0), [], ["q16"])
-    op("G", lambda q: q.iota(T.j16[:, :], [[0, 22], [1, 16]], 0, 0), [], ["j16"])
-    op("G", lambda q: q.affine_select(T.et[:, :], T.one[:, :], [[1, 4], [-4, 128], [-1, 4]], A.is_equal, 0.0, 0, 4), ["one"], ["et"])
-    op("V", lambda q: q.tensor_scalar(T.dd[:, :], T.jj[:, :], 15, None, A.bitwise_and), ["jj"], ["dd"])
-    op("V", lambda q: q.tensor_scalar(T.c1[:, :], T.dd[:, :], 1.0, BIG - 1.0, A.is_equal, A.mult), ["dd"], ["c1"])
-    op("V", lambda q: q.tensor_scalar(T.ck[:, :], T.dd[:, :], 0.0, None, A.is_gt), ["dd"], ["ck"])
-    op("V", lambda q: q.tensor_scalar(T.wt[:, 1:2], T.dd[:, 15:16], 0.0, 1.0 - 1.0 / BIG, A.is_equal, A.mult), ["dd"], ["wt1"])
-    op("V", lambda q: q.tensor_copy(T.uo[:, :], T.uoi[:, :]), ["uoi"], ["uo"])
-    op("V", lambda q: q.tensor_tensor(T.ck[:, :], T.c1[:, :], T.ck[:, :], A.add), ["c1", "ck"], ["ck"])
+    op("G", lambda q: q.iota(T.jm[:, :], [[0, 22], [1, 16]], 0, 0, allow_small_or_imprecise_dtypes=True), [], ["jm"])
+    op("G", lambda q: q.iota(T.idx[:, :], [[1, C]], 0, 0, allow_small_or_imprecise_dtypes=True), [], ["idx"])
+    op("G", lambda q: q.iota(T.q16[:, 66:82], [[1, 2], [16, 8]], 0, 0), [], ["uoi"])
+    for p in range(4):
+        op("G", lambda q: q.affine_select(T.et[:, 512 * p + p:512 * p + 512:4], T.one[:, :], [[-1, 128]], A.is_equal, 0.0, 0, 1), ["one", "et"], [("et_%d" % p)])
+    op("G", lambda q: q.iota(T.q16[:, 0:66], [[0, 3], [16, 22]], 352, 0), [], ["q16"])
+    op("V", lambda q: q.tensor_scalar(T.pm[:, :], T.pm[:, :], 15, None, A.bitwise_and), ["pm"], ["pm"])
+    op("V", lambda q: q.tensor_scalar(T.wt[:, 2:3], T.pm[:, 0:1], -1.0, None, A.mult), ["pm"], ["wt2"])
+    op("V", lambda q: q.tensor_scalar(T.wt[:, 3:4], T.pm[:, 0:1], 1.0, None, A.add), ["pm"], ["wt3"])
+    op("V", lambda q: q.tensor_scalar(T.wt[:, 1:2], T.pm[:, 0:1], 15.0, 1.0 - 1.0 / BIG, A.is_equal, A.mult), ["pm"], ["wt1"])
+    op("V", lambda q: q.tensor_scalar(T.gm[:, 0:C], T.jm[:, :], T.wt[:, 3:4], BIG - 1.0, A.is_equal, A.mult), ["jm", "wt3"], ["gm"])
+    op("S", lambda q: q.activation(T.am[:, :], T.jm[:, :], F.Abs, bias=T.wt[:, 2:3]), ["jm", "wt2"], ["am"])
+    op("S", lambda q: q.activation(T.ck[:, :], T.am[:, :], sign), ["am"], ["ck"])
     op("V", lambda q: q.tensor_scalar(T.wt[:, 0:1], T.wt[:, 1:2], 1.0 / BIG, None, A.add), ["wt1"], ["wt0"])
 
     op("V", lambda q: q.tensor_copy(T.pp16[:, :], T.ppi[:, :]), ["ppi"], ["pp16"])
     op("V", lambda q: q.tensor_copy(T.pr16[:, :], T.pri[:, :]), ["pri"], ["pr16"])
     op("S", lambda q: q.activation(T.rep0[:, 0:C], T.idx[:, :].indirect(T.pp16[:, 0:22]), copy), ["pp16", "idx"], [("rep0", 0, C)])
     op("V", lambda q: q.tensor_copy(T.rf16[:, :], T.rfi[:, :]), ["rfi"], ["rf16"])
-    op("V", lambda q: q.tensor_copy(T.rep0[:, C:2 * C], T.idx[:, :].indirect(T.rf16[:, 0:22])), ["rf16", "idx"], [("rep0", C, 2 * C)])
+    op("V", lambda q: q.tensor_copy(T.uo[:, :], T.q16[:, 66:82]), ["uoi"], ["uo"])
+    op("V", lambda q: q.quantize_mx(T.uq[:, :], T.us[:, :], T.ut[:, :]), ["ut"], ["uq"])
+    op("V", lambda q: q.tensor_copy(T.ua[:, 0:256].bitcast(dt.uint32), T.uq[:, 0:128].bitcast(dt.uint32).indirect(T.uo[:, 0:16])), ["uq", "uo"], ["ua"])
+    op("S", lambda q: q.activation(T.uas[:, 0:256], T.us[:, 0:128].indirect(T.uo[:, 0:16]), copy), ["uq", "uo"], ["uas"])
 
     def quant(t, i, buf, keys):
         a, b = CH[i]
         op("V", lambda q: q.quantize_mx(T["xq%d" % t][:, a:b], T["xs%d" % t][:, a:b], T[buf][:, 4 * a:4 * b]), keys, [("xq%d" % t, a, b)])
-
-    op("V", lambda q: q.quantize_mx(T.uq[:, :], T.us[:, :], T.ut[:, :]), ["ut"], ["uq"])
-    op("V", lambda q: q.tensor_copy(T.ua[:, 0:256].bitcast(dt.uint32), T.uq[:, 0:128].bitcast(dt.uint32).indirect(T.uo[:, 0:16])), ["uq", "uo"], ["ua"])
-    op("V", lambda q: q.tensor_copy(T.uas[:, 0:256], T.us[:, 0:128].indirect(T.uo[:, 0:16])), ["uq", "uo"], ["uas"])
 
     def mm(bank, side, scale, c0, rq, rs, a, b, rd):
         op("P", lambda q: q.matmul_mx(T["b%d" % bank][:, 0:b - a], T[side][:, c0:c0 + 128], T[scale][:, c0:c0 + 128],
@@ -267,10 +268,9 @@ def rank_program(g, core, T, topo):
                 unpack(t, p, *CH[1])
                 evac(p, *CH[1])
 
-    def compose(t, rep):
-        k = T.pr16[:, 22 * t:22 * t + 22]
-        op("S", lambda q: q.activation(T.pkf[:, 0:C], T[rep][:, 0:C].indirect(k), copy), ["pr16", (rep, 0, C)], [("pkf", 0, C)])
-        op("S", lambda q: q.activation(T.pkf[:, C:2 * C], T[rep][:, C:2 * C].indirect(k), copy), ["pr16", (rep, C, 2 * C)], [("pkf", C, 2 * C)])
+    def compose(t, rep, n):
+        k, a, b = T.pr16[:, 22 * t:22 * t + 22], C * n, C * n + C
+        op("S", lambda q: q.activation(T.pkf[:, a:b], T[rep][:, a:b].indirect(k), copy), ["pr16", (rep, a, b)], [("pkf", a, b)])
 
     def kplus(t, q0):
         k = T.pr16[:, 22 * t:22 * t + 22]
@@ -282,14 +282,20 @@ def rank_program(g, core, T, topo):
     def scan(out, okey, lo, fac, data, dkey):
         op("V", lambda q: q.tensor_tensor_scan(T[out][:, lo:lo + C], T[fac][:, :], data, 0.0, A.mult, A.add), [fac, dkey], [(okey, lo, lo + C)])
 
-    def finish_lists(t, psrc, pkey, fsrc, fkey):
-        ba, di = "ba%d" % t, "di%d" % t
+    def lists_base(t, psrc, pkey, fsrc, fkey):
+        ba = "ba%d" % t
         for n, (s, key) in enumerate(((psrc, pkey), (fsrc, fkey), (fsrc, fkey))):
             op("V", lambda q: q.tensor_copy(T[ba][:, 22 * n:22 * n + 22], s), [key], [(ba, 22 * n, 22 * n + 22)])
-        scan("sp", "sp", 0, "ck", T.pkf[:, 0:C], ("pkf", 0, C))
-        scan("sp", "sp", C, "ck", T.pkf[:, C:2 * C], ("pkf", C, 2 * C))
-        op("V", lambda q: q.tensor_scalar(T.x1[:, 0:44], T.sp[:, 15:2 * C:16], T.wt[:, 0:1], None, A.mult), ["sp", "wt0"], [("x1", 0, 44)])
-        op("V", lambda q: q.tensor_copy(T.pka[:, 22 * t:22 * t + 22], T.x1[:, 0:22]), [("x1", 0, 22)], ["pk16%d" % t])
+
+    def lists_scan(t, n):
+        a, b = C * n, C * n + C
+        scan("sp", "sp", a, "ck", T.pkf[:, a:b], ("pkf", a, b))
+        op("V", lambda q: q.tensor_scalar(T.x1[:, 22 * n:22 * n + 22], T.sp[:, a + 15:b:16], T.wt[:, 0:1], None, A.mult), [("sp", a, b), "wt0"], [("x1", 22 * n, 22 * n + 22)])
+        if n == 0:
+            op("V", lambda q: q.tensor_copy(T.pka[:, 22 * t:22 * t + 22], T.x1[:, 0:22]), [("x1", 0, 22)], ["pk16%d" % t])
+
+    def lists_rest(t):
+        ba, di = "ba%d" % t, "di%d" % t
         op("V", lambda q: q.tensor_tensor(T.xx[:, :], T.x1[:, 22:44], T.qk[:, 22 * t:22 * t + 22], A.add), [("x1", 22, 44), "qk"], ["xx"])
         op("V", lambda q: q.tensor_scalar(T.nn[:, :], T.xx[:, :], 1.0 / 352, 0.4986, A.mult, A.subtract), ["xx"], ["nn"])
         op("V", lambda q: q.tensor_scalar(T.nn[:, :], T.nn[:, :], -352.0, None, A.mult), ["nn"], ["nn"])
@@ -297,20 +303,26 @@ def rank_program(g, core, T, topo):
         op("V", lambda q: q.tensor_tensor(T[di][:, :], T.x1[:, :], T[ba][:, :], A.subtract), ["x1", ba], [di])
         op("V", lambda q: q.tensor_scalar(T[ba][:, 22:44], T[ba][:, 22:44], 512.0, None, A.add), [(ba, 22, 44)], [(ba, 22, 44)])
 
-    kplus(0, "V")
-    compose(0, "rep0")
     quant(0, 0, "xin", ["xin0"])
-    op("V", lambda q: q.quantize_mx(T.eq[:, :], T.es[:, :], T.et[:, :]), ["et"], ["eq"])
     quant(0, 1, "xin", ["xin1"])
+    op("V", lambda q: q.tensor_copy(T.rep0[:, C:2 * C], T.idx[:, :].indirect(T.rf16[:, 0:22])), ["rf16", "idx"], [("rep0", C, 2 * C)])
+    kplus(0, "V")
+    compose(0, "rep0", 0)
+    compose(0, "rep0", 1)
+    op("S", lambda q: q.activation(T.mk[:, 0:C], T.am[:, :], F.Relu, bias=4096.0, scale=-4096.0), ["am"], [("mk", 0, C)])
+    op("S", lambda q: q.activation(T.mk[:, C:2 * C], T.am[:, :], F.Relu, bias=1.0, scale=-1.0), ["am"], [("mk", C, 2 * C)])
+    op("S", lambda q: q.activation(T.c01[:, :], T.jm[:, :], sign), ["jm"], ["c01"])
+    op("S", lambda q: q.activation(T.c0b[:, :], T.jm[:, :], sign), ["jm"], ["c0b"])
+    op("V", lambda q: q.quantize_mx(T.eq[:, :], T.es[:, :], T.et[:, :]), ["et"] + ["et_%d" % p for p in range(4)], ["eq"])
     head(0, 0)
     head(0, 1)
-    op("V", lambda q: q.tensor_scalar(T.pm[:, :], T.pm[:, :], 15, None, A.bitwise_and), ["pm"], ["pm"])
-    op("V", lambda q: q.tensor_tensor(T.qq[:, :], T.pm[:, :], T.q16[:, :], A.add), ["pm", "q16"], ["qq"])
+    op("V", lambda q: q.tensor_tensor(T.ck[:, :], T.gm[:, 0:C], T.ck[:, :], A.add), ["gm", "ck"], ["ck"])
+    op("V", lambda q: q.tensor_tensor(T.qq[:, :], T.pm[:, :], T.q16[:, 0:66], A.add), ["pm", "q16"], ["qq"])
     op("V", lambda q: q.tensor_tensor(T.qk[:, :], T.qq[:, :], T.pri[:, :], A.subtract), ["qq", "pri"], ["qk"])
-    finish_lists(0, T.ppi[:, :], "ppi", T.rfi[:, :], "rfi")
-    op("V", lambda q: q.tensor_scalar(T.mk[:, 0:C], T.dd[:, :], 0.0, 4096.0, A.is_equal, A.mult), ["dd"], [("mk", 0, C)])
-    op("V", lambda q: q.tensor_scalar(T.mk[:, C:2 * C], T.dd[:, :], 0.0, None, A.is_equal), ["dd"], [("mk", C, 2 * C)])
-    op("V", lambda q: q.tensor_scalar(T.c01[:, :], T.j16[:, :], 1.0, None, A.min), ["j16"], ["c01"])
+    lists_base(0, T.ppi[:, :], "ppi", T.rfi[:, :], "rfi")
+    lists_scan(0, 0)
+    lists_scan(0, 1)
+    lists_rest(0)
 
     p16, p16key = T.pp16[:, 0:22], "pp16"
     for t in range(3):
@@ -332,13 +344,17 @@ def rank_program(g, core, T, topo):
         op("V", lambda q: q.tensor_copy(T[oc][:, :], T[sel][:, 0:44]), [(sel, 0, 44)], [oc])
         for p in range(4):
             op("S", lambda q: q.activation(T.gp[:, C * p:C * p + C], T.fp[:, C * p:C * p + C].indirect(T[oc][:, 0:22]), copy, scale=0.5), ["fp%d" % p, oc], ["gp%d" % p])
-        op("V", lambda q: q.tensor_tensor(T.gm[:, :], T.bw[:, :].indirect(T[oc][:, 0:44]), T.mk[:, :], A.mult), ["bw", oc, "mk"], ["gm"])
+        for p in range(3):
+            a, b = C * p + H, C * p + C
+            op("G", lambda q: q.affine_select(T.g2[:, a:b], T.gp[:, a:b], [[0, H]], A.is_ge, 0.0, 1, 0), ["gp%d" % p], [("g2", a, b)])
+        op("V", lambda q: q.tensor_tensor(T.gm[:, C:2 * C], T.bw[:, :].indirect(T[oc][:, 22:44]), T.mk[:, C:2 * C], A.mult), ["bw", oc, "mk"], ["gm"])
+        op("V", lambda q: q.tensor_tensor(T.gb[:, :], T.bw[:, 0:C].indirect(T[oc][:, 0:22]), T.mk[:, 0:C], A.mult), [("bw", 0, C), oc, "mk"], ["gb"])
         eqs(2)
         choose(44, 66)
-        scan("gs", "gs", 0, "c01", T.gm[:, 0:C], "gm")
         scan("gs", "gs", C, "c01", T.gm[:, C:2 * C], "gm")
+        scan("gsb", "gsb", 0, "c0b", T.gb[:, :], "gb")
         op("V", lambda q: q.tensor_tensor(T.tt[:, 0:22], T.gs[:, C + 15:2 * C:16], T[sel][:, 22:44], A.max), ["gs", sel], ["t1"])
-        op("V", lambda q: q.tensor_tensor(T.tt[:, 22:44], T.gs[:, 15:C:16], T.tt[:, 0:22], A.min), ["gs", "t1"], ["t2"])
+        op("V", lambda q: q.tensor_tensor(T.tt[:, 22:44], T.gsb[:, 15:C:16], T.tt[:, 0:22], A.min), ["gsb", "t1"], ["t2"])
         op("V", lambda q: q.tensor_tensor(T.t3[:, :], T.tt[:, 22:44], T[sel][:, 44:66], A.max), ["t2", sel], ["t3"])
         op("V", lambda q: q.tensor_scalar(fi_, T.t3[:, :], 511, None, A.bitwise_and), ["t3"], [fi])
         op("V", lambda q: q.tensor_copy(fu_, T.fia[:, 22 * t + 11:22 * t + 22]), [fi], [fu])
@@ -351,7 +367,9 @@ def rank_program(g, core, T, topo):
             zq, zs = "%sq%d" % (nm, t), "%ss%d" % (nm, t)
             for p in range(4):
                 a, b = C * p + o, C * p + o + H
-                if half == 0:
+                if half == 0 and p < 3:
+                    continue
+                elif half == 0:
                     op("V", lambda q: q.tensor_copy(T.g2[:, a:b], T.gp[:, a:b]), ["gp%d" % p], [("g2", a, b)])
                 else:
                     op("S", lambda q: q.activation(T.g2[:, a:b], T.gp[:, a:b], copy), ["gp%d" % p], [("g2", a, b)])
@@ -364,37 +382,63 @@ def rank_program(g, core, T, topo):
                 sends([zq], k, lambda: send(g, T, topo, core, dst, T["zrq%d" % t][:, 0:H].bitcast(dt.uint8), T[zq][:, 0:H].bitcast(dt.uint8), "za%d" % t))
                 sends([zq], k, lambda: send(g, T, topo, core, dst, T["zrs%d" % t][:, 0:H], T[zs][:, 0:H], "za%d" % t))
             elif half == 0:
-                cd, sc = [], []
-                for h, c in enumerate(hp):
-                    rid, pid = topo.addr(c, core)
-                    m = bits(topo, core, c, 8, 8 * h)[0]
-                    lo, hi = h * H // 2, (h + 1) * H // 2
-                    cd.append(RemoteDMATransfer(dst_ids=[DstId(rid=rid, pnc=pid)], dma_engine_mask=m, remote_sem=T.sem.hca, src=T[zq][:, lo:hi].bitcast(dt.uint8), dst=T.hq[:, 0:H // 2].bitcast(dt.uint8)))
-                    sc.append(RemoteDMATransfer(dst_ids=[DstId(rid=rid, pnc=pid)], dma_engine_mask=m, remote_sem=T.sem.hsa, src=T[zs][:, lo:hi], dst=T.hs[:, 0:H // 2]))
-                sends([zq], 8 * len(hp), lambda: g.remote_dma_fused(cd, local_sem=T.sem.rl))
-                sends([zq], 8 * len(hp), lambda: g.remote_dma_fused(sc, local_sem=T.sem.rl))
+                sends([zq], bits(topo, core, hp[0])[1], lambda: send(g, T, topo, core, hp[0], T.hq[:, 0:H].bitcast(dt.uint8), T[zq][:, 0:H].bitcast(dt.uint8), "hca"))
+                sends([zq], bits(topo, core, hp[-1])[1], lambda: send(g, T, topo, core, hp[-1], T.hs[:, 0:H], T[zs][:, 0:H], "hsa"))
         rep = "rep%d" % (t + 1)
         op("S", lambda q: q.activation(T[rep][:, 0:C], T.idx[:, :].indirect(T[oc][:, 0:22]), copy), [oc, "idx"], [(rep, 0, C)])
         op("S", lambda q: q.activation(T[rep][:, C:2 * C], T.idx[:, :].indirect(T[f16][:, 0:22]), copy), [f16, "idx"], [(rep, C, 2 * C)])
         for p in range(4):
             mm(4 + p, "wq", "wsp", 128 * p, "zlq%d" % t, "zls%d" % t, 0, H, ["wq", "wsp", "zlq%d" % t])
-        op("S", lambda q: q.activation(T.fsr[:, :], T.idx[:, :].indirect(T["fs%d" % t][:, 0:22]), copy), ["fs%d" % t, "idx"], ["fsr"])
-        op("S", lambda q: q.activation(T.hr[:, :], T.fsr[:, :].indirect(T[f16][:, 0:22]), copy), ["fsr", f16], ["hr"])
-        for p in range(4):
-            op("S", lambda q: q.activation(T.bp[:, C * p:C * p + H], T["b%d" % (4 + p)][:, 0:H], copy, scale=0.03125), [], ["b%d" % (4 + p), ("bp%d" % p, 0, H)])
-        op("V", lambda q: q.tensor_copy(T.ew[:, :].indirect(T[oc][:, 0:22]), T.hr[:, :]), ["hr", oc], ["ew"])
-        scan("esc", "esc", 0, "ck", T.ew[:, :], "ew")
-        op("V", lambda q: q.tensor_scalar(T.ei[:, :], T.esc[:, 15:C:16], T.wt[:, 0:1], None, A.mult), ["esc", "wt0"], ["ei"])
-        op("V", lambda q: q.tensor_copy(e_, T.ei[:, :]), ["ei"], ["e16%d" % t])
-
-        def next_lists():
-            finish_lists(t + 1, T[sel][:, 0:22], (sel, 0, 22), fi_, fi)
-        if t < 2 and not LATE[t]:
-            kplus(t + 1, "S")
-            compose(t + 1, rep)
-            next_lists()
         if t == 0:
+            compose(t + 1, rep, 0)
+
+        def own_half():
+            for p in range(4):
+                op("S", lambda q: q.activation(T.bp[:, C * p:C * p + H], T["b%d" % (4 + p)][:, 0:H], copy, scale=0.03125), [], ["b%d" % (4 + p), ("bp%d" % p, 0, H)])
+
+        def theirs():
+            op("S", lambda q: q.activation(T.fsr[:, :], T.idx[:, :].indirect(T["fs%d" % t][:, 0:22]), copy), ["fs%d" % t, "idx"], ["fsr"])
+
+        def wrapped(src, key, out, okey):
+            scan("esc", "esc", 0, "ck", src, key)
+            op("V", lambda q: q.tensor_scalar(T.ei[:, :], T.esc[:, 15:C:16], T.wt[:, 0:1], None, A.mult), ["esc", "wt0"], ["ei"])
+            op("V", lambda q: q.tensor_copy(out, T.ei[:, :]), ["ei"], [okey])
+
+        def inverse(src, key):
+            op("V", lambda q: q.tensor_copy(T.ew[:, :].indirect(T[oc][:, 0:22]), src), [key, oc], ["ew"])
+        if t < 2:
+            theirs()
+            op("S", lambda q: q.activation(T.hr[:, :], T.fsr[:, :].indirect(T[f16][:, 0:22]), copy), ["fsr", f16], ["hr"])
+            if t == 0:
+                compose(t + 1, rep, 1)
+            own_half()
+        else:
+            inverse(T.idx[:, :], "idx")
+            wrapped(T.ew[:, :], "ew", T.rf16[:, :], "rf16")
+            own_half()
+            op("S", lambda q: q.activation(T.hr[:, :], T[rep][:, C:2 * C].indirect(T.rf16[:, 0:22]), copy), [(rep, C, 2 * C), "rf16"], ["hr"])
+            wrapped(T.hr[:, :], "hr", T.pp16[:, :], "pp16")
+            theirs()
+            op("S", lambda q: q.activation(T.pkf[:, 0:C], T.fsr[:, :].indirect(T.pp16[:, 0:22]), copy), ["fsr", "pp16"], [("pkf", 0, C)])
+        if t < 2:
+            lists_base(t + 1, T[sel][:, 0:22], (sel, 0, 22), fi_, fi)
+            kplus(t + 1, "S")
+        if t == 0:
+            lists_scan(t + 1, 0)
+        if t == 1:
+            compose(t + 1, rep, 0)
+        if t == 2:
             op("V", lambda q: q.quantize_mx(T.vq[:, :], T.vs[:, :], T.vt[:, :]), ["vt"], ["vq"])
+        if t < 2:
+            inverse(T.hr[:, :], "hr")
+            wrapped(T.ew[:, :], "ew", e_, "e16%d" % t)
+        else:
+            wrapped(T.pkf[:, 0:C], ("pkf", 0, C), e_, "e16%d" % t)
+
+        if t < 2:
+            lists_scan(t + 1, 1 - t)
+        for p in range(4 - XS[t], 4):
+            unpack(t, p, 0, C)
         if t == 2:
             dma("Y", T.pf[:, :], T[rep][0:128:16, :], [rep], ["pf"])
         for p in range(4):
@@ -404,11 +448,18 @@ def rank_program(g, core, T, topo):
                 op("S", lambda q: q.activation(o, i_, copy, scale=0.03125), [], ["b%d" % p, ("bp%d" % p, H, C)])
             else:
                 op("V", lambda q: q.tensor_scalar(o, i_, 0.03125, None, A.mult), [], ["b%d" % p, ("bp%d" % p, H, C)])
-        if t < 2 and LATE[t]:
-            kplus(t + 1, "S")
-            compose(t + 1, rep)
+        for i, (a, b) in enumerate(CH):
+            e = T.e16a[:, 22 * t + a // 16:22 * t + b // 16]
+            for p in range(4 - XS[t], 4):
+                op("S", lambda q: q.activation(T.bg[:, C * p + a:C * p + b], T.bp[:, C * p:C * p + C].indirect(e), copy), ["bp%d" % p, "e16%d" % t], [("bg%d" % p, a, b)])
+        if t == 1:
+            compose(t + 1, rep, 1)
         for i, (a, b) in enumerate(CH):
             for p in range(4):
+                if p >= 4 - XS[t]:
+                    op("V", lambda q: q.tensor_tensor(T.xt[:, 4 * a + p:4 * b:4], T["b%d" % (4 + p)][:, a:b], T.bg[:, C * p + a:C * p + b], A.add),
+                       [("bg%d" % p, a, b)], ["b%d" % (4 + p), ("xt%d" % p, a, b)])
+                    continue
                 op("V", lambda q: q.tensor_tensor(T.xt[:, 4 * a + p:4 * b:4], T.bp[:, C * p:C * p + C].indirect(T.e16a[:, 22 * t + a // 16:22 * t + b // 16]), T.fp[:, C * p + a:C * p + b], A.add),
                    ["bp%d" % p, "e16%d" % t, ("fp%d" % p, a, b)], [("xt%d" % p, a, b)])
             quant(t + 1, i, "xt", [("xt%d" % p, a, b) for p in range(4)])
@@ -422,7 +473,9 @@ def rank_program(g, core, T, topo):
                 dma("S", T.y[:, a:b], T.yt[:, a:b], [("yt", a, b)], ["yout%d" % i])
                 for k in range(4):
                     dma("Y" if k < 3 else "S", T.osc[4 * k:4 * k + 4, a:b], T[xs][32 * k:32 * k + 4, a:b], [(xq, a, b)], ["oscout%d%d" % (i, k)])
-        if t < 2 and LATE[t]:
-            next_lists()
+        if t == 1:
+            lists_scan(t + 1, 1)
+        if t < 2:
+            lists_rest(t + 1)
         p16, p16key = T[oc][:, 0:22], oc
     finish()

@@ -1,10 +1,16 @@
+from concourse.bass import DstId, RemoteDMATransfer
 from concourse.mybir import dt, AluOpType, ActivationFunctionType
 
 A, F = AluOpType, ActivationFunctionType
 N, C, H = 8, 352, 176
 STEP = [4, 1, 2]
 CH = [(0, 224), (224, 352)]
-XS = [2, 2, 2]
+SEQ = [("PFbpfTHOKh", "", "r"), ("PbpTHOh", "FK", "fr"), ("iOCcTEve", "", "")]
+CUT = ((0, 11), (11, 22))
+EARLY = ()
+POOL = ()
+EV = ()
+XS = [1, 1, 1]
 BIG = 16384.0
 
 SCRATCH = {
@@ -164,9 +170,10 @@ def hand_on(g, core, T, topo):
             if core not in hp:
                 continue
             t, k = STEP.index(s), bits(topo, src, core)[1]
-            if core == hp[-1]:
-                g.wait_ge(T.sem.hla, k)
-                n[0] += send(g, T, topo, core, dst, T["fs%d" % t][:, 0:22], T.hl[:, 0:22], "la%d" % t)
+            mine = [ab for c, ab in zip((hp[0], hp[-1]), CUT) if c == core]
+            g.wait_ge(T.sem.hla, 8 * len(mine))
+            for a, b in mine:
+                n[0] += send(g, T, topo, core, dst, T["fs%d" % t][:, a:b], T.hl[:, a:b], "la%d" % t)
             if core == hp[0]:
                 g.wait_ge(T.sem.hca, k)
                 n[0] += send(g, T, topo, core, dst, T["zrq%d" % t][:, 0:H].bitcast(dt.uint8), T.hq[:, 0:H].bitcast(dt.uint8), "za%d" % t)
@@ -188,7 +195,7 @@ def rank_program(g, core, T, topo):
         src = T.cores[rank ^ STEP[t]]
         hp = helpers(T, topo, src, core)
         if hp:
-            lands("fs%d" % t, "la%d" % t, bits(topo, hp[-1], core)[1])
+            lands("fs%d" % t, "la%d" % t, bits(topo, hp[0], core)[1] + bits(topo, hp[-1], core)[1])
             lands("zr%d" % t, "za%d" % t, bits(topo, hp[0], core)[1] + bits(topo, hp[-1], core)[1])
         else:
             lands("fs%d" % t, "la%d" % t, bits(topo, src, core)[1])
@@ -206,22 +213,30 @@ def rank_program(g, core, T, topo):
 
     op("V", lambda q: q.memset(T.one[:, :], 1.0), [], ["one"])
     op("V", lambda q: q.memset(T.et[:, :], 0.0), [], ["et"])
-    op("V", lambda q: q.memset(T.bw[:, 352:512], 0.0), [], [("bw", 352, 512)])
+    for nm, a, b, v in (("c01", 0, C, 1.0), ("bw", 352, 512, 0.0)):
+        op("V", lambda q: q.memset(T[nm][:, a:b], v), [], [(nm, a, b)])
     op("G", lambda q: q.iota(T.pm[:, :], [[0, 66]], 0, 1), [], ["pm"])
-    op("G", lambda q: q.iota(T.jm[:, :], [[0, 22], [1, 16]], 0, 0, allow_small_or_imprecise_dtypes=True), [], ["jm"])
+    op("G", lambda q: q.iota(T.gs[:, 0:16], [[1, 16]], 0, 0, allow_small_or_imprecise_dtypes=True), [], ["gs"])
     op("G", lambda q: q.iota(T.idx[:, :], [[1, C]], 0, 0, allow_small_or_imprecise_dtypes=True), [], ["idx"])
     op("G", lambda q: q.iota(T.q16[:, 66:82], [[1, 2], [16, 8]], 0, 0), [], ["uoi"])
     for p in range(4):
         op("G", lambda q: q.affine_select(T.et[:, 512 * p + p:512 * p + 512:4], T.one[:, :], [[-1, 128]], A.is_equal, 0.0, 0, 1), ["one", "et"], [("et_%d" % p)])
-    op("G", lambda q: q.iota(T.q16[:, 0:66], [[0, 3], [16, 22]], 352, 0), [], ["q16"])
+    op("G", lambda q: q.iota(T.q16[:, 0:66], [[0, 3], [16, 22]], 352 - 512, 0), [], ["q16"])
+    op("G", lambda q: q.iota(T.jm[:, :], [[0, 22], [1, 16]], 0, 0, allow_small_or_imprecise_dtypes=True), [], ["jm"])
+    op("G", lambda q: q.affine_select(T.c01[:, :], T.c01[:, :], [[0, 22], [1, 16]], A.is_gt, 0.0, 0, 0), ["c01"], ["c01"])
     op("V", lambda q: q.tensor_scalar(T.pm[:, :], T.pm[:, :], 15, None, A.bitwise_and), ["pm"], ["pm"])
-    op("V", lambda q: q.tensor_scalar(T.wt[:, 2:3], T.pm[:, 0:1], -1.0, None, A.mult), ["pm"], ["wt2"])
     op("V", lambda q: q.tensor_scalar(T.wt[:, 3:4], T.pm[:, 0:1], 1.0, None, A.add), ["pm"], ["wt3"])
+    op("V", lambda q: q.tensor_scalar(T.wt[:, 2:3], T.pm[:, 0:1], -1.0, None, A.mult), ["pm"], ["wt2"])
+    op("V", lambda q: q.tensor_copy(T.wt[:, 4:5], T.pm[:, 0:1]), ["pm"], ["wt4"])
+    op("V", lambda q: q.tensor_scalar(T.gm[:, 0:16], T.gs[:, 0:16], T.wt[:, 3:4], BIG - 1.0, A.is_equal, A.mult), ["gs", "wt3"], [("gm", 0, 16)])
+    op("V", lambda q: q.tensor_copy(T.e16a[:, 0:22], T.pm[:, 0:22]), ["pm"], ["e160"])
+    op("V", lambda q: q.tensor_scalar(T.gm[:, 16:32], T.gs[:, 0:16], T.wt[:, 4:5], None, A.not_equal), ["gs", "wt4"], [("gm", 16, 32)])
     op("V", lambda q: q.tensor_scalar(T.wt[:, 1:2], T.pm[:, 0:1], 15.0, 1.0 - 1.0 / BIG, A.is_equal, A.mult), ["pm"], ["wt1"])
-    op("V", lambda q: q.tensor_scalar(T.gm[:, 0:C], T.jm[:, :], T.wt[:, 3:4], BIG - 1.0, A.is_equal, A.mult), ["jm", "wt3"], ["gm"])
-    op("S", lambda q: q.activation(T.am[:, :], T.jm[:, :], F.Abs, bias=T.wt[:, 2:3]), ["jm", "wt2"], ["am"])
-    op("S", lambda q: q.activation(T.ck[:, :], T.am[:, :], sign), ["am"], ["ck"])
+    op("V", lambda q: q.tensor_tensor(T.gm[:, 32:48], T.gm[:, 0:16], T.gm[:, 16:32], A.add), [("gm", 0, 32)], [("gm", 32, 48)])
+    op("S", lambda q: q.activation(T.ck[:, :], T.gm[:, 32:48].indirect(T.e16a[:, 0:22]), copy), [("gm", 32, 48), "e160"], ["ck"])
+    op("V", lambda q: q.tensor_scalar(T.gm[:, 48:64], T.gs[:, 0:16], T.wt[:, 3:4], 15.0, A.is_equal, A.mult), ["gs", "wt3"], [("gm", 48, 64)])
     op("V", lambda q: q.tensor_scalar(T.wt[:, 0:1], T.wt[:, 1:2], 1.0 / BIG, None, A.add), ["wt1"], ["wt0"])
+    op("V", lambda q: q.tensor_tensor(T.gm[:, 64:80], T.gm[:, 48:64], T.gm[:, 16:32], A.add), [("gm", 16, 64)], [("gm", 64, 80)])
 
     op("V", lambda q: q.tensor_copy(T.pp16[:, :], T.ppi[:, :]), ["ppi"], ["pp16"])
     op("V", lambda q: q.tensor_copy(T.pr16[:, :], T.pri[:, :]), ["pri"], ["pr16"])
@@ -256,15 +271,17 @@ def rank_program(g, core, T, topo):
 
     def head(t, i):
         signs(t, i)
-        if i == 0:
-            for p in (0, 1):
+        for p in range(4):
+            if i == 0 and p in EARLY:
                 unpack(t, p, *CH[0])
+            elif i == 1 and p in EARLY:
                 evac(p, *CH[0])
-        else:
-            for p in (2, 3):
+        for p in range(4):
+            if i == 1 and p not in EARLY:
                 unpack(t, p, 0, C)
                 evac(p, 0, C)
-            for p in (0, 1):
+        for p in range(4):
+            if i == 1 and p in EARLY:
                 unpack(t, p, *CH[1])
                 evac(p, *CH[1])
 
@@ -285,23 +302,31 @@ def rank_program(g, core, T, topo):
     def lists_base(t, psrc, pkey, fsrc, fkey):
         ba = "ba%d" % t
         for n, (s, key) in enumerate(((psrc, pkey), (fsrc, fkey), (fsrc, fkey))):
-            op("V", lambda q: q.tensor_copy(T[ba][:, 22 * n:22 * n + 22], s), [key], [(ba, 22 * n, 22 * n + 22)])
+            op("V", lambda q: q.tensor_scalar(T[ba][:, 22 * n:22 * n + 22], s, 512.0 if n == 1 else 0.0, None, A.add), [key], [(ba, 22 * n, 22 * n + 22)])
 
     def lists_scan(t, n):
         a, b = C * n, C * n + C
         scan("sp", "sp", a, "ck", T.pkf[:, a:b], ("pkf", a, b))
-        op("V", lambda q: q.tensor_scalar(T.x1[:, 22 * n:22 * n + 22], T.sp[:, a + 15:b:16], T.wt[:, 0:1], None, A.mult), [("sp", a, b), "wt0"], [("x1", 22 * n, 22 * n + 22)])
+        op("V", lambda q: q.tensor_scalar(T.x1[:, 22 * n:22 * n + 22], T.sp[:, a + 15:b:16], T.wt[:, 0:1], 512.0 * n, A.mult, A.add), [("sp", a, b), "wt0"], [("x1", 22 * n, 22 * n + 22)])
         if n == 0:
-            op("V", lambda q: q.tensor_copy(T.pka[:, 22 * t:22 * t + 22], T.x1[:, 0:22]), [("x1", 0, 22)], ["pk16%d" % t])
+            op("V", lambda q: q.tensor_scalar(T.pka[:, 22 * t:22 * t + 22], T.sp[:, a + 15:b:16], T.wt[:, 0:1], None, A.mult), [("sp", a, b), "wt0"], ["pk16%d" % t])
+
+    def rest(t, n):
+        ba, di = "ba%d" % t, "di%d" % t
+        if n == 0:
+            op("V", lambda q: q.tensor_tensor(T.xx[:, :], T.x1[:, 22:44], T.qk[:, 22 * t:22 * t + 22], A.add), [("x1", 22, 44), "qk"], ["xx"])
+        if n == 1:
+            op("V", lambda q: q.tensor_scalar(T.nn[:, :], T.xx[:, :], 1.0 / 352, 0.4986, A.mult, A.subtract), ["xx"], ["nn"])
+        if n == 2:
+            op("V", lambda q: q.tensor_scalar(T.nn[:, :], T.nn[:, :], -352.0, None, A.mult), ["nn"], ["nn"])
+        if n == 3:
+            op("V", lambda q: q.tensor_tensor(T.x1[:, 44:66], T.xx[:, :], T.nn[:, :], A.add), ["xx", "nn"], [("x1", 44, 66)])
+        if n == 4:
+            op("V", lambda q: q.tensor_tensor(T[di][:, :], T.x1[:, :], T[ba][:, :], A.subtract), ["x1", ba], [di])
 
     def lists_rest(t):
-        ba, di = "ba%d" % t, "di%d" % t
-        op("V", lambda q: q.tensor_tensor(T.xx[:, :], T.x1[:, 22:44], T.qk[:, 22 * t:22 * t + 22], A.add), [("x1", 22, 44), "qk"], ["xx"])
-        op("V", lambda q: q.tensor_scalar(T.nn[:, :], T.xx[:, :], 1.0 / 352, 0.4986, A.mult, A.subtract), ["xx"], ["nn"])
-        op("V", lambda q: q.tensor_scalar(T.nn[:, :], T.nn[:, :], -352.0, None, A.mult), ["nn"], ["nn"])
-        op("V", lambda q: q.tensor_tensor(T.x1[:, 44:66], T.xx[:, :], T.nn[:, :], A.add), ["xx", "nn"], [("x1", 44, 66)])
-        op("V", lambda q: q.tensor_tensor(T[di][:, :], T.x1[:, :], T[ba][:, :], A.subtract), ["x1", ba], [di])
-        op("V", lambda q: q.tensor_scalar(T[ba][:, 22:44], T[ba][:, 22:44], 512.0, None, A.add), [(ba, 22, 44)], [(ba, 22, 44)])
+        rest(t, 0)
+        rest(t, 1)
 
     quant(0, 0, "xin", ["xin0"])
     quant(0, 1, "xin", ["xin1"])
@@ -309,14 +334,13 @@ def rank_program(g, core, T, topo):
     kplus(0, "V")
     compose(0, "rep0", 0)
     compose(0, "rep0", 1)
-    op("S", lambda q: q.activation(T.mk[:, 0:C], T.am[:, :], F.Relu, bias=4096.0, scale=-4096.0), ["am"], [("mk", 0, C)])
-    op("S", lambda q: q.activation(T.mk[:, C:2 * C], T.am[:, :], F.Relu, bias=1.0, scale=-1.0), ["am"], [("mk", C, 2 * C)])
-    op("S", lambda q: q.activation(T.c01[:, :], T.jm[:, :], sign), ["jm"], ["c01"])
-    op("S", lambda q: q.activation(T.c0b[:, :], T.jm[:, :], sign), ["jm"], ["c0b"])
     op("V", lambda q: q.quantize_mx(T.eq[:, :], T.es[:, :], T.et[:, :]), ["et"] + ["et_%d" % p for p in range(4)], ["eq"])
     head(0, 0)
     head(0, 1)
-    op("V", lambda q: q.tensor_tensor(T.ck[:, :], T.gm[:, 0:C], T.ck[:, :], A.add), ["gm", "ck"], ["ck"])
+    op("S", lambda q: q.activation(T.hr[:, :], T.jm[:, :], F.Abs, bias=T.wt[:, 2:3]), ["jm", "wt2"], ["hr"])
+    op("S", lambda q: q.activation(T.mk[:, C:2 * C], T.hr[:, :], F.Relu, bias=1.0, scale=-1.0), ["hr"], [("mk", C, 2 * C)])
+    op("S", lambda q: q.activation(T.c0b[:, :], T.gm[:, 64:80].indirect(T.e16a[:, 0:22]), copy), [("gm", 64, 80), "e160"], ["c0b"])
+
     op("V", lambda q: q.tensor_tensor(T.qq[:, :], T.pm[:, :], T.q16[:, 0:66], A.add), ["pm", "q16"], ["qq"])
     op("V", lambda q: q.tensor_tensor(T.qk[:, :], T.qq[:, :], T.pri[:, :], A.subtract), ["qq", "pri"], ["qk"])
     lists_base(0, T.ppi[:, :], "ppi", T.rfi[:, :], "rfi")
@@ -329,8 +353,11 @@ def rank_program(g, core, T, topo):
         fi_, fu_, e_ = T.fia[:, 22 * t:22 * t + 22], T.fua[:, 12 * t:12 * t + 11], T.e16a[:, 22 * t:22 * t + 22]
         ba, di, oc, sel, f16, fu, fi = [n + str(t) for n in ("ba", "di", "oc", "sel", "f16", "fu", "fi")]
         op("V", lambda q: q.tensor_tensor(T.am[:, :], T.sa[:, :].indirect(p16), T.mra[:, C * t:C * t + C], A.mult), ["sa", p16key, "mr%d" % t], ["am"])
+        rest(t, 2)
         op("V", lambda q: q.tensor_tensor(T.bw[:, 512:864], T.sa[:, :].indirect(T.pka[:, 22 * t:22 * t + 22]), T.am[:, :], A.mult), ["sa", "pk16%d" % t, "am"], [("bw", 512, 864)])
+        rest(t, 3)
         scan("sE", "sE", 0, "ck", T.bw[:, 512:864], ("bw", 512, 864))
+        rest(t, 4)
 
         def eqs(n):
             op("V", lambda q: q.tensor_scalar(T.e3[:, 22 * n:22 * n + 22], T.sE[:, 15:C:16], 0.0, None, A.is_gt), ["sE"], [("e3", 22 * n, 22 * n + 22)])
@@ -342,17 +369,15 @@ def rank_program(g, core, T, topo):
         eqs(1)
         choose(0, 44)
         op("V", lambda q: q.tensor_copy(T[oc][:, :], T[sel][:, 0:44]), [(sel, 0, 44)], [oc])
+        op("S", lambda q: q.activation(T.gb[:, :], T.bw[:, 0:C].indirect(T[oc][:, 0:22]), copy, scale=4096.0), [("bw", 0, C), oc], ["gb"])
         for p in range(4):
             op("S", lambda q: q.activation(T.gp[:, C * p:C * p + C], T.fp[:, C * p:C * p + C].indirect(T[oc][:, 0:22]), copy, scale=0.5), ["fp%d" % p, oc], ["gp%d" % p])
-        for p in range(3):
-            a, b = C * p + H, C * p + C
-            op("G", lambda q: q.affine_select(T.g2[:, a:b], T.gp[:, a:b], [[0, H]], A.is_ge, 0.0, 1, 0), ["gp%d" % p], [("g2", a, b)])
         op("V", lambda q: q.tensor_tensor(T.gm[:, C:2 * C], T.bw[:, :].indirect(T[oc][:, 22:44]), T.mk[:, C:2 * C], A.mult), ["bw", oc, "mk"], ["gm"])
-        op("V", lambda q: q.tensor_tensor(T.gb[:, :], T.bw[:, 0:C].indirect(T[oc][:, 0:22]), T.mk[:, 0:C], A.mult), [("bw", 0, C), oc, "mk"], ["gb"])
         eqs(2)
-        choose(44, 66)
         scan("gs", "gs", C, "c01", T.gm[:, C:2 * C], "gm")
+        op("V", lambda q: q.tensor_tensor(T.sm[:, 44:66], T.e3[:, 44:66], T[di][:, 44:66], A.mult), [("e3", 44, 66), di], [("sm", 44, 66)])
         scan("gsb", "gsb", 0, "c0b", T.gb[:, :], "gb")
+        op("V", lambda q: q.tensor_tensor(T[sel][:, 44:66], T.sm[:, 44:66], T[ba][:, 44:66], A.add), [("sm", 44, 66), ba], [(sel, 44, 66)])
         op("V", lambda q: q.tensor_tensor(T.tt[:, 0:22], T.gs[:, C + 15:2 * C:16], T[sel][:, 22:44], A.max), ["gs", sel], ["t1"])
         op("V", lambda q: q.tensor_tensor(T.tt[:, 22:44], T.gsb[:, 15:C:16], T.tt[:, 0:22], A.min), ["gsb", "t1"], ["t2"])
         op("V", lambda q: q.tensor_tensor(T.t3[:, :], T.tt[:, 22:44], T[sel][:, 44:66], A.max), ["t2", sel], ["t3"])
@@ -361,19 +386,28 @@ def rank_program(g, core, T, topo):
         op("V", lambda q: q.tensor_copy(T[f16][:, :], fi_), [fi], [f16])
         dst = T.cores[rank ^ STEP[t]]
         hp = helpers(T, topo, core, dst)
-        far = hp[-1] if hp else dst
-        sends([f16], bits(topo, core, far)[1], lambda: send(g, T, topo, core, far, T.hl[:, 0:22] if hp else T["fs%d" % t][:, 0:22], T[f16][:, 0:22], "hla" if hp else "la%d" % t))
+        if hp:
+            halves = []
+            for n, (c, (a, b)) in enumerate(zip((hp[0], hp[-1]), CUT)):
+                rid, pid = topo.addr(c, core)
+                halves.append(RemoteDMATransfer(dst_ids=[DstId(rid=rid, pnc=pid)], dma_engine_mask=bits(topo, core, c, 8, 8 * n)[0],
+                                                remote_sem=T.sem.hla, src=T[f16][:, a:b], dst=T.hl[:, a:b]))
+            sends([f16], 16, lambda: g.remote_dma_fused(halves, local_sem=T.sem.rl))
+        else:
+            sends([f16], bits(topo, core, dst)[1], lambda: send(g, T, topo, core, dst, T["fs%d" % t][:, 0:22], T[f16][:, 0:22], "la%d" % t))
+        for p in POOL:
+            a, b = C * p, C * p + H
+            op("G", lambda q: q.affine_select(T.g2[:, a:b], T.gp[:, a:b], [[0, H]], A.is_ge, 0.0, 1, 0), ["gp%d" % p], [("g2", a, b)])
         for half, (buf, off, o, nm) in enumerate((("ztu", fu_, H, "zu"), ("ztl", T[f16][:, 0:11], 0, "zl"))):
             zq, zs = "%sq%d" % (nm, t), "%ss%d" % (nm, t)
             for p in range(4):
                 a, b = C * p + o, C * p + o + H
-                if half == 0 and p < 3:
-                    continue
-                elif half == 0:
-                    op("V", lambda q: q.tensor_copy(T.g2[:, a:b], T.gp[:, a:b]), ["gp%d" % p], [("g2", a, b)])
-                else:
+                if half == 1 and p not in POOL:
                     op("S", lambda q: q.activation(T.g2[:, a:b], T.gp[:, a:b], copy), ["gp%d" % p], [("g2", a, b)])
             for p in range(4):
+                for n in ((0, 1), (2,), (3,), ())[p] if half == 0 else ():
+                    a, b = C * n + o, C * n + o + H
+                    op("V", lambda q: q.tensor_copy(T.g2[:, a:b], T.gp[:, a:b]), ["gp%d" % n], [("g2", a, b)])
                 a, b = C * p + o, C * p + o + H
                 op("V", lambda q: q.tensor_tensor(T[buf][:, p:4 * H:4], T.gp[:, C * p:C * p + C].indirect(off), T.g2[:, a:b], A.add), ["gp%d" % p, ("g2", a, b), f16, fu], ["%s_%d" % (buf, p)])
             op("V", lambda q: q.quantize_mx(T[zq][:, :], T[zs][:, :], T[buf][:, :]), ["%s_%d" % (buf, p) for p in range(4)], [zq])
@@ -389,9 +423,6 @@ def rank_program(g, core, T, topo):
         op("S", lambda q: q.activation(T[rep][:, C:2 * C], T.idx[:, :].indirect(T[f16][:, 0:22]), copy), [f16, "idx"], [(rep, C, 2 * C)])
         for p in range(4):
             mm(4 + p, "wq", "wsp", 128 * p, "zlq%d" % t, "zls%d" % t, 0, H, ["wq", "wsp", "zlq%d" % t])
-        if t == 0:
-            compose(t + 1, rep, 0)
-
         def own_half():
             for p in range(4):
                 op("S", lambda q: q.activation(T.bp[:, C * p:C * p + H], T["b%d" % (4 + p)][:, 0:H], copy, scale=0.03125), [], ["b%d" % (4 + p), ("bp%d" % p, 0, H)])
@@ -401,42 +432,38 @@ def rank_program(g, core, T, topo):
 
         def wrapped(src, key, out, okey):
             scan("esc", "esc", 0, "ck", src, key)
-            op("V", lambda q: q.tensor_scalar(T.ei[:, :], T.esc[:, 15:C:16], T.wt[:, 0:1], None, A.mult), ["esc", "wt0"], ["ei"])
-            op("V", lambda q: q.tensor_copy(out, T.ei[:, :]), ["ei"], [okey])
+            op("V", lambda q: q.tensor_scalar(out, T.esc[:, 15:C:16], T.wt[:, 0:1], None, A.mult), ["esc", "wt0"], [okey])
 
         def inverse(src, key):
             op("V", lambda q: q.tensor_copy(T.ew[:, :].indirect(T[oc][:, 0:22]), src), [key, oc], ["ew"])
-        if t < 2:
-            theirs()
+
+        def by_place():
             op("S", lambda q: q.activation(T.hr[:, :], T.fsr[:, :].indirect(T[f16][:, 0:22]), copy), ["fsr", f16], ["hr"])
-            if t == 0:
-                compose(t + 1, rep, 1)
-            own_half()
-        else:
+
+        def by_column():
+            op("S", lambda q: q.activation(T.hr[:, :], T[rep][:, C:2 * C].indirect(T.rf16[:, 0:22]), copy), [(rep, C, 2 * C), "rf16"], ["hr"])
+
+        def looked_up():
+            op("S", lambda q: q.activation(T.hr[:, :], T.fsr[:, :].indirect(T.pp16[:, 0:22]), copy), ["fsr", "pp16"], ["hr"])
+
+        def place_of():
             inverse(T.idx[:, :], "idx")
             wrapped(T.ew[:, :], "ew", T.rf16[:, :], "rf16")
-            own_half()
-            op("S", lambda q: q.activation(T.hr[:, :], T[rep][:, C:2 * C].indirect(T.rf16[:, 0:22]), copy), [(rep, C, 2 * C), "rf16"], ["hr"])
-            wrapped(T.hr[:, :], "hr", T.pp16[:, :], "pp16")
-            theirs()
-            op("S", lambda q: q.activation(T.pkf[:, 0:C], T.fsr[:, :].indirect(T.pp16[:, 0:22]), copy), ["fsr", "pp16"], [("pkf", 0, C)])
-        if t < 2:
-            lists_base(t + 1, T[sel][:, 0:22], (sel, 0, 22), fi_, fi)
-            kplus(t + 1, "S")
-        if t == 0:
-            lists_scan(t + 1, 0)
-        if t == 1:
-            compose(t + 1, rep, 0)
-        if t == 2:
-            op("V", lambda q: q.quantize_mx(T.vq[:, :], T.vs[:, :], T.vt[:, :]), ["vt"], ["vq"])
-        if t < 2:
+
+        def to_columns():
             inverse(T.hr[:, :], "hr")
             wrapped(T.ew[:, :], "ew", e_, "e16%d" % t)
-        else:
-            wrapped(T.pkf[:, 0:C], ("pkf", 0, C), e_, "e16%d" % t)
-
-        if t < 2:
-            lists_scan(t + 1, 1 - t)
+        parts = {
+            "P": lambda: compose(t + 1, rep, 0), "p": lambda: lists_scan(t + 1, 0),
+            "F": lambda: compose(t + 1, rep, 1), "f": lambda: lists_scan(t + 1, 1),
+            "b": lambda: lists_base(t + 1, T[sel][:, 0:22], (sel, 0, 22), fi_, fi), "K": lambda: kplus(t + 1, "S"), "r": lambda: lists_rest(t + 1),
+            "i": place_of, "C": by_column, "c": lambda: wrapped(T.hr[:, :], "hr", T.pp16[:, :], "pp16"),
+            "T": theirs, "E": looked_up, "e": lambda: wrapped(T.hr[:, :], "hr", e_, "e16%d" % t),
+            "H": by_place, "h": to_columns, "O": own_half,
+            "v": lambda: op("V", lambda q: q.quantize_mx(T.vq[:, :], T.vs[:, :], T.vt[:, :]), ["vt"], ["vq"]),
+        }
+        for n in SEQ[t][0]:
+            parts[n]()
         for p in range(4 - XS[t], 4):
             unpack(t, p, 0, C)
         if t == 2:
@@ -444,7 +471,7 @@ def rank_program(g, core, T, topo):
         for p in range(4):
             mm(p, "wq", "wsp", 128 * p, "zrq%d" % t, "zrs%d" % t, 0, H, ["wq", "wsp", "zr%d" % t])
             o, i_ = T.bp[:, C * p + H:C * p + C], T["b%d" % p][:, 0:H]
-            if p % 2 == 0:
+            if p not in EV:
                 op("S", lambda q: q.activation(o, i_, copy, scale=0.03125), [], ["b%d" % p, ("bp%d" % p, H, C)])
             else:
                 op("V", lambda q: q.tensor_scalar(o, i_, 0.03125, None, A.mult), [], ["b%d" % p, ("bp%d" % p, H, C)])
@@ -452,8 +479,8 @@ def rank_program(g, core, T, topo):
             e = T.e16a[:, 22 * t + a // 16:22 * t + b // 16]
             for p in range(4 - XS[t], 4):
                 op("S", lambda q: q.activation(T.bg[:, C * p + a:C * p + b], T.bp[:, C * p:C * p + C].indirect(e), copy), ["bp%d" % p, "e16%d" % t], [("bg%d" % p, a, b)])
-        if t == 1:
-            compose(t + 1, rep, 1)
+        for n in SEQ[t][1]:
+            parts[n]()
         for i, (a, b) in enumerate(CH):
             for p in range(4):
                 if p >= 4 - XS[t]:
@@ -473,9 +500,7 @@ def rank_program(g, core, T, topo):
                 dma("S", T.y[:, a:b], T.yt[:, a:b], [("yt", a, b)], ["yout%d" % i])
                 for k in range(4):
                     dma("Y" if k < 3 else "S", T.osc[4 * k:4 * k + 4, a:b], T[xs][32 * k:32 * k + 4, a:b], [(xq, a, b)], ["oscout%d%d" % (i, k)])
-        if t == 1:
-            lists_scan(t + 1, 1)
-        if t < 2:
-            lists_rest(t + 1)
+        for n in SEQ[t][2]:
+            parts[n]()
         p16, p16key = T[oc][:, 0:22], oc
     finish()

from concourse.bass import DstId, RemoteDMATransfer
from concourse.mybir import dt, AluOpType, ActivationFunctionType

A, F = AluOpType, ActivationFunctionType
N, C, H = 8, 352, 176
STEP = [4, 1, 2]
CH = [(0, 224), (224, 352)]
SEQ = [("PFbpfTHOKh", "", "r"), ("PbpTHOh", "FK", "fr"), ("iOCcTEve", "", "")]
CUT = ((0, 11), (11, 22))
EARLY = ()
POOL = ()
EV = ()
XS = [1, 1, 1]
BIG = 16384.0

SCRATCH = {
    "xin": ("sbuf", [128, 4 * C], "bfloat16"), "xt": ("sbuf", [128, 4 * C], "bfloat16"),
    "ut": ("sbuf", [128, 512], "bfloat16"), "vt": ("sbuf", [128, 512], "bfloat16"),
    "uq": ("sbuf", [128, 128], "float8_e4m3fn_x4"), "us": ("sbuf", [128, 128], "uint8"),
    "ua": ("sbuf", [128, 256], "float8_e4m3fn_x4"), "uas": ("sbuf", [128, 256], "uint8"),
    "vq": ("sbuf", [128, 128], "float8_e4m3fn_x4"), "vs": ("sbuf", [128, 128], "uint8"),
    "wq": ("sbuf", [128, 512], "float8_e4m3fn_x4"), "wsp": ("sbuf", [128, 512], "uint8"),
    "one": ("sbuf", [128, 128], "bfloat16"), "gb": ("sbuf", [128, C], "bfloat16"), "gsb": ("sbuf", [128, C], "bfloat16"), "c0b": ("sbuf", [128, C], "bfloat16"),
    "bg": ("sbuf", [128, 4 * C], "bfloat16"), "et": ("sbuf", [128, 2048], "bfloat16"),
    "eq": ("sbuf", [128, 512], "float8_e4m3fn_x4"), "es": ("sbuf", [128, 512], "uint8"),
    "ppi": ("sbuf", [128, 22], "int32"), "rfi": ("sbuf", [128, 22], "int32"), "pri": ("sbuf", [128, 66], "int32"),
    "pp16": ("sbuf", [128, 22], "uint16"), "rf16": ("sbuf", [128, 22], "uint16"), "pr16": ("sbuf", [128, 66], "uint16"),
    "idx": ("sbuf", [128, C], "float32"), "jm": ("sbuf", [128, C], "float32"), "mk": ("sbuf", [128, 2 * C], "float32"),
    "ck": ("sbuf", [128, C], "float32"), "c01": ("sbuf", [128, C], "float32"),
    "wt": ("sbuf", [128, 8], "float32"), "uo": ("sbuf", [128, 16], "uint16"),
    "pm": ("sbuf", [128, 66], "int32"), "q16": ("sbuf", [128, 82], "int32"),
    "qq": ("sbuf", [128, 66], "int32"), "qk": ("sbuf", [128, 66], "float32"),
    "sa": ("sbuf", [128, C], "bfloat16"), "bw": ("sbuf", [128, 864], "float32"), "am": ("sbuf", [128, C], "float32"),
    "sE": ("sbuf", [128, C], "float32"), "e3": ("sbuf", [128, 66], "float32"), "sm": ("sbuf", [128, 66], "float32"),
    "gm": ("sbuf", [128, 2 * C], "float32"), "gs": ("sbuf", [128, 2 * C], "float32"),
    "tt": ("sbuf", [128, 44], "float32"), "t3": ("sbuf", [128, 22], "int32"),
    "pkf": ("sbuf", [128, 2 * C], "float32"), "sp": ("sbuf", [128, 2 * C], "float32"),
    "x1": ("sbuf", [128, 66], "int32"), "xx": ("sbuf", [128, 22], "float32"), "nn": ("sbuf", [128, 22], "int32"),
    "fsr": ("sbuf", [128, C], "float32"), "hr": ("sbuf", [128, C], "float32"), "ew": ("sbuf", [128, C], "float32"),
    "esc": ("sbuf", [128, C], "float32"), "ei": ("sbuf", [128, 22], "int32"),
    "fp": ("sbuf", [128, 4 * C], "bfloat16"), "gp": ("sbuf", [128, 4 * C], "bfloat16"), "bp": ("sbuf", [128, 4 * C], "bfloat16"),
    "ztu": ("sbuf", [128, 4 * H], "bfloat16"), "ztl": ("sbuf", [128, 4 * H], "bfloat16"),
    "yt": ("sbuf", [128, C], "float32"), "g2": ("sbuf", [128, 4 * C], "bfloat16"),
}
for k in range(8):
    SCRATCH["b%d" % k] = ("psum", [128, 512], "float32")
for k in range(4):
    SCRATCH["xq%d" % k] = ("sbuf", [128, C], "float8_e4m3fn_x4")
    SCRATCH["xs%d" % k] = ("sbuf", [128, C], "uint8")
for k in range(3):
    for nm in ("zu", "zl", "zr"):
        SCRATCH["%sq%d" % (nm, k)] = ("sbuf", [128, H], "float8_e4m3fn_x4")
        SCRATCH["%ss%d" % (nm, k)] = ("sbuf", [128, H], "uint8")
    SCRATCH["oc%d" % k] = ("sbuf", [128, 44], "uint16")
    SCRATCH["f16%d" % k] = ("sbuf", [128, 22], "uint16")
    SCRATCH["fs%d" % k] = ("sbuf", [128, 22], "uint16")
    SCRATCH["sel%d" % k] = ("sbuf", [128, 66], "float32")
    SCRATCH["ba%d" % k] = ("sbuf", [128, 66], "float32")
    SCRATCH["di%d" % k] = ("sbuf", [128, 66], "float32")
    SCRATCH["rep%d" % k] = ("sbuf", [128, 2 * C], "float32")
SCRATCH["fia"] = ("sbuf", [128, 66], "int32")
SCRATCH["pka"] = ("sbuf", [128, 66], "uint16")
SCRATCH["e16a"] = ("sbuf", [128, 66], "uint16")
SCRATCH["fua"] = ("sbuf", [128, 36], "uint16")
SCRATCH["mra"] = ("sbuf", [128, 3 * C], "float32")
SCRATCH["rep3"] = ("sbuf", [128, 2 * C], "float32")
SCRATCH["hq"] = ("sbuf", [128, H], "float8_e4m3fn_x4")
SCRATCH["hs"] = ("sbuf", [128, H], "uint8")
SCRATCH["hl"] = ("sbuf", [128, 22], "uint16")

ENG = {"V": "sv", "S": "ss", "P": "st", "G": "sg"}
SEMAPHORES = ["sv", "ss", "st", "sg", "rl", "hla", "hca", "hsa"] + ["la%d" % k for k in range(3)] + ["za%d" % k for k in range(3)] + ["d%d" % k for k in range(40)]


def machine(g, T):
    queues = {"V": g.vector, "S": g.scalar, "P": g.tensor, "G": g, "Y": g.sync}
    know = {q: {} for q in queues}
    cnt, hist, behind, ndma = {}, {}, {}, [0]

    def need(q, tok):
        sem, val = tok
        k = know[q]
        if k.get(sem, 0) >= val:
            return
        queues[q].wait_ge(T.sem[sem], val)
        k[sem] = val
        for s, v in behind.get(tok, {}).items():
            k[s] = max(k.get(s, 0), v)

    def norm(rs):
        return [(r, 0, 1 << 30) if isinstance(r, str) else r for r in rs]

    def before(q, rd, wr):
        toks = []
        for key, lo, hi in rd:
            toks += [tok for (l, h, tok, w) in hist.get(key, []) if w and l < hi and lo < h]
        for key, lo, hi in wr:
            toks += [tok for (l, h, tok, w) in hist.get(key, []) if l < hi and lo < h]
        best = {}
        for s, v in toks:
            best[s] = max(best.get(s, 0), v)
        own = ENG.get(q)
        for s in sorted(best, key=lambda s: s == own):
            need(q, (s, best[s]))

    def after(tok, rd, wr):
        for key, lo, hi in wr:
            hist[key] = [e for e in hist.get(key, []) if not (lo <= e[0] and e[1] <= hi)] + [(lo, hi, tok, True)]
        for key, lo, hi in rd:
            hist.setdefault(key, []).append((lo, hi, tok, False))

    def op(q, call, rd, wr):
        rd, wr = norm(rd), norm(wr)
        before(q, rd, wr)
        sem = ENG[q]
        cnt[sem] = cnt.get(sem, 0) + 1
        tok = (sem, cnt[sem])
        call(queues[q]).then_inc(T.sem[sem], 1)
        behind[tok] = dict(know[q])
        after(tok, rd, wr)

    def dma(q, out, in_, rd, wr):
        rd, wr = norm(rd), norm(wr)
        before(q, rd, wr)
        sem = "d%d" % ndma[0]
        ndma[0] += 1
        cnt[sem] = 16
        queues[q].dma_start(out, in_).then_inc(T.sem[sem], 16)
        behind[(sem, 16)] = dict(know[q])
        after((sem, 16), rd, wr)

    def lands(key, sem, val):
        after((sem, val), [], norm([key]))

    def sends(rd, n, call):
        before("G", norm(rd), [])
        call()
        cnt["rl"] = cnt.get("rl", 0) + n

    def finish():
        for s in sorted(cnt, key=lambda s: s[0] == "d"):
            need("Y", (s, cnt[s]))
    return op, dma, lands, sends, finish


def bits(topo, src, dst, n=16, skip=0):
    e = topo.engines(src, dst)[skip:skip + n]
    return sum(1 << i for i in e), len(e)


def helpers(T, topo, src, dst):
    if topo.may_write(src, dst):
        return []
    return [c for c in topo.cores_of(src) if c not in T.cores and topo.die(c) == topo.die(src) and topo.may_write(c, dst)][:2]


def send(g, T, topo, src, dst, out, in_, rsem, n=16):
    rid, pid = topo.addr(dst, src)
    m, k = bits(topo, src, dst, n)
    g.remote_dma(out_ap=out, in_ap=in_, remote_sem=T.sem[rsem], local_sem=T.sem.rl, pid=pid, routing_id=rid, dma_engine_mask=m)
    return k


def hand_on(g, core, T, topo):
    n = [0]
    for r, src in enumerate(T.cores):
        for s in STEP:
            dst = T.cores[r ^ s]
            hp = helpers(T, topo, src, dst)
            if core not in hp:
                continue
            t, k = STEP.index(s), bits(topo, src, core)[1]
            mine = [ab for c, ab in zip((hp[0], hp[-1]), CUT) if c == core]
            g.wait_ge(T.sem.hla, 8 * len(mine))
            for a, b in mine:
                n[0] += send(g, T, topo, core, dst, T["fs%d" % t][:, a:b], T.hl[:, a:b], "la%d" % t)
            if core == hp[0]:
                g.wait_ge(T.sem.hca, k)
                n[0] += send(g, T, topo, core, dst, T["zrq%d" % t][:, 0:H].bitcast(dt.uint8), T.hq[:, 0:H].bitcast(dt.uint8), "za%d" % t)
            if core == hp[-1]:
                g.wait_ge(T.sem.hsa, k)
                n[0] += send(g, T, topo, core, dst, T["zrs%d" % t][:, 0:H], T.hs[:, 0:H], "za%d" % t)
    if n[0]:
        g.wait_ge(T.sem.rl, n[0])


def rank_program(g, core, T, topo):
    rank = T.rank_of(core)
    if rank is None:
        return hand_on(g, core, T, topo)
    op, dma, lands, sends, finish = machine(g, T)
    copy, sign = F.Copy, F.Sign

    for t in range(3):
        src = T.cores[rank ^ STEP[t]]
        hp = helpers(T, topo, src, core)
        if hp:
            lands("fs%d" % t, "la%d" % t, bits(topo, hp[0], core)[1] + bits(topo, hp[-1], core)[1])
            lands("zr%d" % t, "za%d" % t, bits(topo, hp[0], core)[1] + bits(topo, hp[-1], core)[1])
        else:
            lands("fs%d" % t, "la%d" % t, bits(topo, src, core)[1])
            lands("zr%d" % t, "za%d" % t, 2 * bits(topo, src, core)[1])

    for i, (a, b) in enumerate(CH):
        dma("Y", T.xin[:, 4 * a:4 * b], T.x[:, 4 * a:4 * b], [], ["xin%d" % i])
    dma("S", T.ppi[:, :], T.pp[:, :], [], ["ppi"])
    dma("S", T.pri[:, :], T.pr[:, :], [], ["pri"])
    dma("S", T.ut[:, :], T.u[:, :], [], ["ut"])
    dma("S", T.rfi[:, :], T.rf[:, :], [], ["rfi"])
    dma("Y", T.wq[:, 0:512].bitcast(dt.uint8), T.wc[:, :], [], ["wq"])
    dma("Y", T.wsp[:, 0:512], T.ws[:, :], [], ["wsp"])
    dma("Y", T.vt[:, :], T.v[:, :], [], ["vt"])

    op("V", lambda q: q.memset(T.one[:, :], 1.0), [], ["one"])
    op("V", lambda q: q.memset(T.et[:, :], 0.0), [], ["et"])
    for nm, a, b, v in (("c01", 0, C, 1.0), ("bw", 352, 512, 0.0)):
        op("V", lambda q: q.memset(T[nm][:, a:b], v), [], [(nm, a, b)])
    op("G", lambda q: q.iota(T.pm[:, :], [[0, 66]], 0, 1), [], ["pm"])
    op("G", lambda q: q.iota(T.gs[:, 0:16], [[1, 16]], 0, 0, allow_small_or_imprecise_dtypes=True), [], ["gs"])
    op("G", lambda q: q.iota(T.idx[:, :], [[1, C]], 0, 0, allow_small_or_imprecise_dtypes=True), [], ["idx"])
    op("G", lambda q: q.iota(T.q16[:, 66:82], [[1, 2], [16, 8]], 0, 0), [], ["uoi"])
    for p in range(4):
        op("G", lambda q: q.affine_select(T.et[:, 512 * p + p:512 * p + 512:4], T.one[:, :], [[-1, 128]], A.is_equal, 0.0, 0, 1), ["one", "et"], [("et_%d" % p)])
    op("G", lambda q: q.iota(T.q16[:, 0:66], [[0, 3], [16, 22]], 352 - 512, 0), [], ["q16"])
    op("G", lambda q: q.iota(T.jm[:, :], [[0, 22], [1, 16]], 0, 0, allow_small_or_imprecise_dtypes=True), [], ["jm"])
    op("G", lambda q: q.affine_select(T.c01[:, :], T.c01[:, :], [[0, 22], [1, 16]], A.is_gt, 0.0, 0, 0), ["c01"], ["c01"])
    op("V", lambda q: q.tensor_scalar(T.pm[:, :], T.pm[:, :], 15, None, A.bitwise_and), ["pm"], ["pm"])
    op("V", lambda q: q.tensor_scalar(T.wt[:, 3:4], T.pm[:, 0:1], 1.0, None, A.add), ["pm"], ["wt3"])
    op("V", lambda q: q.tensor_scalar(T.wt[:, 2:3], T.pm[:, 0:1], -1.0, None, A.mult), ["pm"], ["wt2"])
    op("V", lambda q: q.tensor_copy(T.wt[:, 4:5], T.pm[:, 0:1]), ["pm"], ["wt4"])
    op("V", lambda q: q.tensor_scalar(T.gm[:, 0:16], T.gs[:, 0:16], T.wt[:, 3:4], BIG - 1.0, A.is_equal, A.mult), ["gs", "wt3"], [("gm", 0, 16)])
    op("V", lambda q: q.tensor_copy(T.e16a[:, 0:22], T.pm[:, 0:22]), ["pm"], ["e160"])
    op("V", lambda q: q.tensor_scalar(T.gm[:, 16:32], T.gs[:, 0:16], T.wt[:, 4:5], None, A.not_equal), ["gs", "wt4"], [("gm", 16, 32)])
    op("V", lambda q: q.tensor_scalar(T.wt[:, 1:2], T.pm[:, 0:1], 15.0, 1.0 - 1.0 / BIG, A.is_equal, A.mult), ["pm"], ["wt1"])
    op("V", lambda q: q.tensor_tensor(T.gm[:, 32:48], T.gm[:, 0:16], T.gm[:, 16:32], A.add), [("gm", 0, 32)], [("gm", 32, 48)])
    op("S", lambda q: q.activation(T.ck[:, :], T.gm[:, 32:48].indirect(T.e16a[:, 0:22]), copy), [("gm", 32, 48), "e160"], ["ck"])
    op("V", lambda q: q.tensor_scalar(T.gm[:, 48:64], T.gs[:, 0:16], T.wt[:, 3:4], 15.0, A.is_equal, A.mult), ["gs", "wt3"], [("gm", 48, 64)])
    op("V", lambda q: q.tensor_scalar(T.wt[:, 0:1], T.wt[:, 1:2], 1.0 / BIG, None, A.add), ["wt1"], ["wt0"])
    op("V", lambda q: q.tensor_tensor(T.gm[:, 64:80], T.gm[:, 48:64], T.gm[:, 16:32], A.add), [("gm", 16, 64)], [("gm", 64, 80)])

    op("V", lambda q: q.tensor_copy(T.pp16[:, :], T.ppi[:, :]), ["ppi"], ["pp16"])
    op("V", lambda q: q.tensor_copy(T.pr16[:, :], T.pri[:, :]), ["pri"], ["pr16"])
    op("S", lambda q: q.activation(T.rep0[:, 0:C], T.idx[:, :].indirect(T.pp16[:, 0:22]), copy), ["pp16", "idx"], [("rep0", 0, C)])
    op("V", lambda q: q.tensor_copy(T.rf16[:, :], T.rfi[:, :]), ["rfi"], ["rf16"])
    op("V", lambda q: q.tensor_copy(T.uo[:, :], T.q16[:, 66:82]), ["uoi"], ["uo"])
    op("V", lambda q: q.quantize_mx(T.uq[:, :], T.us[:, :], T.ut[:, :]), ["ut"], ["uq"])
    op("V", lambda q: q.tensor_copy(T.ua[:, 0:256].bitcast(dt.uint32), T.uq[:, 0:128].bitcast(dt.uint32).indirect(T.uo[:, 0:16])), ["uq", "uo"], ["ua"])
    op("S", lambda q: q.activation(T.uas[:, 0:256], T.us[:, 0:128].indirect(T.uo[:, 0:16]), copy), ["uq", "uo"], ["uas"])

    def quant(t, i, buf, keys):
        a, b = CH[i]
        op("V", lambda q: q.quantize_mx(T["xq%d" % t][:, a:b], T["xs%d" % t][:, a:b], T[buf][:, 4 * a:4 * b]), keys, [("xq%d" % t, a, b)])

    def mm(bank, side, scale, c0, rq, rs, a, b, rd):
        op("P", lambda q: q.matmul_mx(T["b%d" % bank][:, 0:b - a], T[side][:, c0:c0 + 128], T[scale][:, c0:c0 + 128],
                                      T[rq][:, a:b], T[rs][:, a:b], True, True), rd, ["b%d" % bank])

    def unpack(t, p, a, b):
        mm(4 + p, "eq", "es", 128 * p, "xq%d" % t, "xs%d" % t, a, b, ["eq", ("xq%d" % t, a, b)])

    def evac(p, a, b):
        op("S", lambda q: q.activation(T.fp[:, C * p + a:C * p + b], T["b%d" % (4 + p)][:, 0:b - a], copy), [], ["b%d" % (4 + p), ("fp%d" % p, a, b)])

    def signs(t, i):
        a, b = CH[i]
        for n in range(2):
            mm(2 * i + n, "ua", "uas", 128 * n, "xq%d" % t, "xs%d" % t, a, b, ["ua", "uas", ("xq%d" % t, a, b)])
        tiny = -(2.0 ** -100)
        op("S", lambda q: q.activation(T.sa[:, a:b], T["b%d" % (2 * i)][:, 0:b - a], sign, bias=tiny), [], ["b%d" % (2 * i), ("sa", a, b)])
        op("S", lambda q: q.activation(T.bw[:, a:b], T["b%d" % (2 * i + 1)][:, 0:b - a], sign, bias=tiny), [], ["b%d" % (2 * i + 1), ("bw", a, b)])

    def head(t, i):
        signs(t, i)
        for p in range(4):
            if i == 0 and p in EARLY:
                unpack(t, p, *CH[0])
            elif i == 1 and p in EARLY:
                evac(p, *CH[0])
        for p in range(4):
            if i == 1 and p not in EARLY:
                unpack(t, p, 0, C)
                evac(p, 0, C)
        for p in range(4):
            if i == 1 and p in EARLY:
                unpack(t, p, *CH[1])
                evac(p, *CH[1])

    def compose(t, rep, n):
        k, a, b = T.pr16[:, 22 * t:22 * t + 22], C * n, C * n + C
        op("S", lambda q: q.activation(T.pkf[:, a:b], T[rep][:, a:b].indirect(k), copy), ["pr16", (rep, a, b)], [("pkf", a, b)])

    def kplus(t, q0):
        k = T.pr16[:, 22 * t:22 * t + 22]
        if q0 == "V":
            op("V", lambda q: q.tensor_scalar(T.mra[:, C * t:C * t + C], T.idx[:, :].indirect(k), 1024.0, None, A.add), ["pr16", "idx"], ["mr%d" % t])
        else:
            op("S", lambda q: q.activation(T.mra[:, C * t:C * t + C], T.idx[:, :].indirect(k), F.Identity, bias=1024.0), ["pr16", "idx"], ["mr%d" % t])

    def scan(out, okey, lo, fac, data, dkey):
        op("V", lambda q: q.tensor_tensor_scan(T[out][:, lo:lo + C], T[fac][:, :], data, 0.0, A.mult, A.add), [fac, dkey], [(okey, lo, lo + C)])

    def lists_base(t, psrc, pkey, fsrc, fkey):
        ba = "ba%d" % t
        for n, (s, key) in enumerate(((psrc, pkey), (fsrc, fkey), (fsrc, fkey))):
            op("V", lambda q: q.tensor_scalar(T[ba][:, 22 * n:22 * n + 22], s, 512.0 if n == 1 else 0.0, None, A.add), [key], [(ba, 22 * n, 22 * n + 22)])

    def lists_scan(t, n):
        a, b = C * n, C * n + C
        scan("sp", "sp", a, "ck", T.pkf[:, a:b], ("pkf", a, b))
        op("V", lambda q: q.tensor_scalar(T.x1[:, 22 * n:22 * n + 22], T.sp[:, a + 15:b:16], T.wt[:, 0:1], 512.0 * n, A.mult, A.add), [("sp", a, b), "wt0"], [("x1", 22 * n, 22 * n + 22)])
        if n == 0:
            op("V", lambda q: q.tensor_scalar(T.pka[:, 22 * t:22 * t + 22], T.sp[:, a + 15:b:16], T.wt[:, 0:1], None, A.mult), [("sp", a, b), "wt0"], ["pk16%d" % t])

    def rest(t, n):
        ba, di = "ba%d" % t, "di%d" % t
        if n == 0:
            op("V", lambda q: q.tensor_tensor(T.xx[:, :], T.x1[:, 22:44], T.qk[:, 22 * t:22 * t + 22], A.add), [("x1", 22, 44), "qk"], ["xx"])
        if n == 1:
            op("V", lambda q: q.tensor_scalar(T.nn[:, :], T.xx[:, :], 1.0 / 352, 0.4986, A.mult, A.subtract), ["xx"], ["nn"])
        if n == 2:
            op("V", lambda q: q.tensor_scalar(T.nn[:, :], T.nn[:, :], -352.0, None, A.mult), ["nn"], ["nn"])
        if n == 3:
            op("V", lambda q: q.tensor_tensor(T.x1[:, 44:66], T.xx[:, :], T.nn[:, :], A.add), ["xx", "nn"], [("x1", 44, 66)])
        if n == 4:
            op("V", lambda q: q.tensor_tensor(T[di][:, :], T.x1[:, :], T[ba][:, :], A.subtract), ["x1", ba], [di])

    def lists_rest(t):
        rest(t, 0)
        rest(t, 1)

    quant(0, 0, "xin", ["xin0"])
    quant(0, 1, "xin", ["xin1"])
    op("V", lambda q: q.tensor_copy(T.rep0[:, C:2 * C], T.idx[:, :].indirect(T.rf16[:, 0:22])), ["rf16", "idx"], [("rep0", C, 2 * C)])
    kplus(0, "V")
    compose(0, "rep0", 0)
    compose(0, "rep0", 1)
    op("V", lambda q: q.quantize_mx(T.eq[:, :], T.es[:, :], T.et[:, :]), ["et"] + ["et_%d" % p for p in range(4)], ["eq"])
    head(0, 0)
    head(0, 1)
    op("S", lambda q: q.activation(T.hr[:, :], T.jm[:, :], F.Abs, bias=T.wt[:, 2:3]), ["jm", "wt2"], ["hr"])
    op("S", lambda q: q.activation(T.mk[:, C:2 * C], T.hr[:, :], F.Relu, bias=1.0, scale=-1.0), ["hr"], [("mk", C, 2 * C)])
    op("S", lambda q: q.activation(T.c0b[:, :], T.gm[:, 64:80].indirect(T.e16a[:, 0:22]), copy), [("gm", 64, 80), "e160"], ["c0b"])

    op("V", lambda q: q.tensor_tensor(T.qq[:, :], T.pm[:, :], T.q16[:, 0:66], A.add), ["pm", "q16"], ["qq"])
    op("V", lambda q: q.tensor_tensor(T.qk[:, :], T.qq[:, :], T.pri[:, :], A.subtract), ["qq", "pri"], ["qk"])
    lists_base(0, T.ppi[:, :], "ppi", T.rfi[:, :], "rfi")
    lists_scan(0, 0)
    lists_scan(0, 1)
    lists_rest(0)

    p16, p16key = T.pp16[:, 0:22], "pp16"
    for t in range(3):
        fi_, fu_, e_ = T.fia[:, 22 * t:22 * t + 22], T.fua[:, 12 * t:12 * t + 11], T.e16a[:, 22 * t:22 * t + 22]
        ba, di, oc, sel, f16, fu, fi = [n + str(t) for n in ("ba", "di", "oc", "sel", "f16", "fu", "fi")]
        op("V", lambda q: q.tensor_tensor(T.am[:, :], T.sa[:, :].indirect(p16), T.mra[:, C * t:C * t + C], A.mult), ["sa", p16key, "mr%d" % t], ["am"])
        rest(t, 2)
        op("V", lambda q: q.tensor_tensor(T.bw[:, 512:864], T.sa[:, :].indirect(T.pka[:, 22 * t:22 * t + 22]), T.am[:, :], A.mult), ["sa", "pk16%d" % t, "am"], [("bw", 512, 864)])
        rest(t, 3)
        scan("sE", "sE", 0, "ck", T.bw[:, 512:864], ("bw", 512, 864))
        rest(t, 4)

        def eqs(n):
            op("V", lambda q: q.tensor_scalar(T.e3[:, 22 * n:22 * n + 22], T.sE[:, 15:C:16], 0.0, None, A.is_gt), ["sE"], [("e3", 22 * n, 22 * n + 22)])

        def choose(a, b):
            op("V", lambda q: q.tensor_tensor(T.sm[:, a:b], T.e3[:, a:b], T[di][:, a:b], A.mult), [("e3", a, b), di], [("sm", a, b)])
            op("V", lambda q: q.tensor_tensor(T[sel][:, a:b], T.sm[:, a:b], T[ba][:, a:b], A.add), [("sm", a, b), ba], [(sel, a, b)])
        eqs(0)
        eqs(1)
        choose(0, 44)
        op("V", lambda q: q.tensor_copy(T[oc][:, :], T[sel][:, 0:44]), [(sel, 0, 44)], [oc])
        op("S", lambda q: q.activation(T.gb[:, :], T.bw[:, 0:C].indirect(T[oc][:, 0:22]), copy, scale=4096.0), [("bw", 0, C), oc], ["gb"])
        for p in range(4):
            op("S", lambda q: q.activation(T.gp[:, C * p:C * p + C], T.fp[:, C * p:C * p + C].indirect(T[oc][:, 0:22]), copy, scale=0.5), ["fp%d" % p, oc], ["gp%d" % p])
        op("V", lambda q: q.tensor_tensor(T.gm[:, C:2 * C], T.bw[:, :].indirect(T[oc][:, 22:44]), T.mk[:, C:2 * C], A.mult), ["bw", oc, "mk"], ["gm"])
        eqs(2)
        scan("gs", "gs", C, "c01", T.gm[:, C:2 * C], "gm")
        op("V", lambda q: q.tensor_tensor(T.sm[:, 44:66], T.e3[:, 44:66], T[di][:, 44:66], A.mult), [("e3", 44, 66), di], [("sm", 44, 66)])
        scan("gsb", "gsb", 0, "c0b", T.gb[:, :], "gb")
        op("V", lambda q: q.tensor_tensor(T[sel][:, 44:66], T.sm[:, 44:66], T[ba][:, 44:66], A.add), [("sm", 44, 66), ba], [(sel, 44, 66)])
        op("V", lambda q: q.tensor_tensor(T.tt[:, 0:22], T.gs[:, C + 15:2 * C:16], T[sel][:, 22:44], A.max), ["gs", sel], ["t1"])
        op("V", lambda q: q.tensor_tensor(T.tt[:, 22:44], T.gsb[:, 15:C:16], T.tt[:, 0:22], A.min), ["gsb", "t1"], ["t2"])
        op("V", lambda q: q.tensor_tensor(T.t3[:, :], T.tt[:, 22:44], T[sel][:, 44:66], A.max), ["t2", sel], ["t3"])
        op("V", lambda q: q.tensor_scalar(fi_, T.t3[:, :], 511, None, A.bitwise_and), ["t3"], [fi])
        op("V", lambda q: q.tensor_copy(fu_, T.fia[:, 22 * t + 11:22 * t + 22]), [fi], [fu])
        op("V", lambda q: q.tensor_copy(T[f16][:, :], fi_), [fi], [f16])
        dst = T.cores[rank ^ STEP[t]]
        hp = helpers(T, topo, core, dst)
        if hp:
            halves = []
            for n, (c, (a, b)) in enumerate(zip((hp[0], hp[-1]), CUT)):
                rid, pid = topo.addr(c, core)
                halves.append(RemoteDMATransfer(dst_ids=[DstId(rid=rid, pnc=pid)], dma_engine_mask=bits(topo, core, c, 8, 8 * n)[0],
                                                remote_sem=T.sem.hla, src=T[f16][:, a:b], dst=T.hl[:, a:b]))
            sends([f16], 16, lambda: g.remote_dma_fused(halves, local_sem=T.sem.rl))
        else:
            sends([f16], bits(topo, core, dst)[1], lambda: send(g, T, topo, core, dst, T["fs%d" % t][:, 0:22], T[f16][:, 0:22], "la%d" % t))
        for p in POOL:
            a, b = C * p, C * p + H
            op("G", lambda q: q.affine_select(T.g2[:, a:b], T.gp[:, a:b], [[0, H]], A.is_ge, 0.0, 1, 0), ["gp%d" % p], [("g2", a, b)])
        for half, (buf, off, o, nm) in enumerate((("ztu", fu_, H, "zu"), ("ztl", T[f16][:, 0:11], 0, "zl"))):
            zq, zs = "%sq%d" % (nm, t), "%ss%d" % (nm, t)
            for p in range(4):
                a, b = C * p + o, C * p + o + H
                if half == 1 and p not in POOL:
                    op("S", lambda q: q.activation(T.g2[:, a:b], T.gp[:, a:b], copy), ["gp%d" % p], [("g2", a, b)])
            for p in range(4):
                for n in ((0, 1), (2,), (3,), ())[p] if half == 0 else ():
                    a, b = C * n + o, C * n + o + H
                    op("V", lambda q: q.tensor_copy(T.g2[:, a:b], T.gp[:, a:b]), ["gp%d" % n], [("g2", a, b)])
                a, b = C * p + o, C * p + o + H
                op("V", lambda q: q.tensor_tensor(T[buf][:, p:4 * H:4], T.gp[:, C * p:C * p + C].indirect(off), T.g2[:, a:b], A.add), ["gp%d" % p, ("g2", a, b), f16, fu], ["%s_%d" % (buf, p)])
            op("V", lambda q: q.quantize_mx(T[zq][:, :], T[zs][:, :], T[buf][:, :]), ["%s_%d" % (buf, p) for p in range(4)], [zq])
            if half == 0 and not hp:
                k = bits(topo, core, dst)[1]
                sends([zq], k, lambda: send(g, T, topo, core, dst, T["zrq%d" % t][:, 0:H].bitcast(dt.uint8), T[zq][:, 0:H].bitcast(dt.uint8), "za%d" % t))
                sends([zq], k, lambda: send(g, T, topo, core, dst, T["zrs%d" % t][:, 0:H], T[zs][:, 0:H], "za%d" % t))
            elif half == 0:
                sends([zq], bits(topo, core, hp[0])[1], lambda: send(g, T, topo, core, hp[0], T.hq[:, 0:H].bitcast(dt.uint8), T[zq][:, 0:H].bitcast(dt.uint8), "hca"))
                sends([zq], bits(topo, core, hp[-1])[1], lambda: send(g, T, topo, core, hp[-1], T.hs[:, 0:H], T[zs][:, 0:H], "hsa"))
        rep = "rep%d" % (t + 1)
        op("S", lambda q: q.activation(T[rep][:, 0:C], T.idx[:, :].indirect(T[oc][:, 0:22]), copy), [oc, "idx"], [(rep, 0, C)])
        op("S", lambda q: q.activation(T[rep][:, C:2 * C], T.idx[:, :].indirect(T[f16][:, 0:22]), copy), [f16, "idx"], [(rep, C, 2 * C)])
        for p in range(4):
            mm(4 + p, "wq", "wsp", 128 * p, "zlq%d" % t, "zls%d" % t, 0, H, ["wq", "wsp", "zlq%d" % t])
        def own_half():
            for p in range(4):
                op("S", lambda q: q.activation(T.bp[:, C * p:C * p + H], T["b%d" % (4 + p)][:, 0:H], copy, scale=0.03125), [], ["b%d" % (4 + p), ("bp%d" % p, 0, H)])

        def theirs():
            op("S", lambda q: q.activation(T.fsr[:, :], T.idx[:, :].indirect(T["fs%d" % t][:, 0:22]), copy), ["fs%d" % t, "idx"], ["fsr"])

        def wrapped(src, key, out, okey):
            scan("esc", "esc", 0, "ck", src, key)
            op("V", lambda q: q.tensor_scalar(out, T.esc[:, 15:C:16], T.wt[:, 0:1], None, A.mult), ["esc", "wt0"], [okey])

        def inverse(src, key):
            op("V", lambda q: q.tensor_copy(T.ew[:, :].indirect(T[oc][:, 0:22]), src), [key, oc], ["ew"])

        def by_place():
            op("S", lambda q: q.activation(T.hr[:, :], T.fsr[:, :].indirect(T[f16][:, 0:22]), copy), ["fsr", f16], ["hr"])

        def by_column():
            op("S", lambda q: q.activation(T.hr[:, :], T[rep][:, C:2 * C].indirect(T.rf16[:, 0:22]), copy), [(rep, C, 2 * C), "rf16"], ["hr"])

        def looked_up():
            op("S", lambda q: q.activation(T.hr[:, :], T.fsr[:, :].indirect(T.pp16[:, 0:22]), copy), ["fsr", "pp16"], ["hr"])

        def place_of():
            inverse(T.idx[:, :], "idx")
            wrapped(T.ew[:, :], "ew", T.rf16[:, :], "rf16")

        def to_columns():
            inverse(T.hr[:, :], "hr")
            wrapped(T.ew[:, :], "ew", e_, "e16%d" % t)
        parts = {
            "P": lambda: compose(t + 1, rep, 0), "p": lambda: lists_scan(t + 1, 0),
            "F": lambda: compose(t + 1, rep, 1), "f": lambda: lists_scan(t + 1, 1),
            "b": lambda: lists_base(t + 1, T[sel][:, 0:22], (sel, 0, 22), fi_, fi), "K": lambda: kplus(t + 1, "S"), "r": lambda: lists_rest(t + 1),
            "i": place_of, "C": by_column, "c": lambda: wrapped(T.hr[:, :], "hr", T.pp16[:, :], "pp16"),
            "T": theirs, "E": looked_up, "e": lambda: wrapped(T.hr[:, :], "hr", e_, "e16%d" % t),
            "H": by_place, "h": to_columns, "O": own_half,
            "v": lambda: op("V", lambda q: q.quantize_mx(T.vq[:, :], T.vs[:, :], T.vt[:, :]), ["vt"], ["vq"]),
        }
        for n in SEQ[t][0]:
            parts[n]()
        for p in range(4 - XS[t], 4):
            unpack(t, p, 0, C)
        if t == 2:
            dma("Y", T.pf[:, :], T[rep][0:128:16, :], [rep], ["pf"])
        for p in range(4):
            mm(p, "wq", "wsp", 128 * p, "zrq%d" % t, "zrs%d" % t, 0, H, ["wq", "wsp", "zr%d" % t])
            o, i_ = T.bp[:, C * p + H:C * p + C], T["b%d" % p][:, 0:H]
            if p not in EV:
                op("S", lambda q: q.activation(o, i_, copy, scale=0.03125), [], ["b%d" % p, ("bp%d" % p, H, C)])
            else:
                op("V", lambda q: q.tensor_scalar(o, i_, 0.03125, None, A.mult), [], ["b%d" % p, ("bp%d" % p, H, C)])
        for i, (a, b) in enumerate(CH):
            e = T.e16a[:, 22 * t + a // 16:22 * t + b // 16]
            for p in range(4 - XS[t], 4):
                op("S", lambda q: q.activation(T.bg[:, C * p + a:C * p + b], T.bp[:, C * p:C * p + C].indirect(e), copy), ["bp%d" % p, "e16%d" % t], [("bg%d" % p, a, b)])
        for n in SEQ[t][1]:
            parts[n]()
        for i, (a, b) in enumerate(CH):
            for p in range(4):
                if p >= 4 - XS[t]:
                    op("V", lambda q: q.tensor_tensor(T.xt[:, 4 * a + p:4 * b:4], T["b%d" % (4 + p)][:, a:b], T.bg[:, C * p + a:C * p + b], A.add),
                       [("bg%d" % p, a, b)], ["b%d" % (4 + p), ("xt%d" % p, a, b)])
                    continue
                op("V", lambda q: q.tensor_tensor(T.xt[:, 4 * a + p:4 * b:4], T.bp[:, C * p:C * p + C].indirect(T.e16a[:, 22 * t + a // 16:22 * t + b // 16]), T.fp[:, C * p + a:C * p + b], A.add),
                   ["bp%d" % p, "e16%d" % t, ("fp%d" % p, a, b)], [("xt%d" % p, a, b)])
            quant(t + 1, i, "xt", [("xt%d" % p, a, b) for p in range(4)])
            if t < 2:
                head(t + 1, i)
            else:
                xq, xs = "xq%d" % 3, "xs%d" % 3
                mm(4 + i, "vq", "vs", 0, xq, xs, a, b, ["vq", (xq, a, b)])
                dma("Y", T.oc[:, 4 * a:4 * b], T[xq][:, a:b].bitcast(dt.uint8), [(xq, a, b)], ["ocout%d" % i])
                op("S", lambda q: q.activation(T.yt[:, a:b], T["b%d" % (4 + i)][:, 0:b - a], copy), [], ["b%d" % (4 + i), ("yt", a, b)])
                dma("S", T.y[:, a:b], T.yt[:, a:b], [("yt", a, b)], ["yout%d" % i])
                for k in range(4):
                    dma("Y" if k < 3 else "S", T.osc[4 * k:4 * k + 4, a:b], T[xs][32 * k:32 * k + 4, a:b], [(xq, a, b)], ["oscout%d%d" % (i, k)])
        for n in SEQ[t][2]:
            parts[n]()
        p16, p16key = T[oc][:, 0:22], oc
    finish()
